import numpy as np
import ml_dtypes


def mxq(x, axis, fmt="e4m3"):
    dtype, down = {"e4m3": (ml_dtypes.float8_e4m3fn, 7), "e5m2": (ml_dtypes.float8_e5m2, 14)}[fmt]
    v = np.moveaxis(np.asarray(x, np.float32).astype(ml_dtypes.bfloat16).astype(np.float64), axis, -1)
    blocks = v.reshape(v.shape[:-1] + (-1, 32))
    amax = np.abs(blocks).max(-1, keepdims=True)
    byte = np.maximum(np.where(amax > 0, np.frexp(amax)[1] - 1 + 127, 0) - down, 1)
    scale = np.exp2(byte - 127.0)
    codes = (blocks / scale).astype(np.float32).astype(dtype).astype(np.float64)
    return np.moveaxis((codes * scale).reshape(v.shape), -1, axis)


WIDE = False


def mx_kscale(k):
    if not WIDE:
        return np.ones(k)
    levels = np.array([10, -10, 5, -5, 0])
    if k % 512:
        return np.exp2(np.random.permutation(np.resize(levels, k // 32))).repeat(32)
    a = np.empty((k // 512, 16))
    for p in range(k // 512):
        a[p, :8] = np.random.permutation(np.resize(levels, 8))
        for g in range(8):
            far = levels[np.abs(levels - a[p, g]) >= 10]
            a[p, g + 8] = far[np.random.randint(len(far))]
    return np.exp2(a.ravel()).repeat(32)


BF16 = ml_dtypes.bfloat16


def bf(x):
    return np.asarray(x, np.float32).astype(BF16)


def f64(x):
    return np.asarray(x).astype(np.float64)


N, E, O, Q, TRIPLES, PER, BITS = 1024, 4, 512, 512, 3, 3, 2
J = TRIPLES * PER
NV = BITS**J
EO = E * O


def calibrate(x, cal):
    low = np.minimum(2.0 * x, 1.0)
    high = np.maximum(2.0 * x - 1.0, 0.0)
    return cal * low + (1.0 - cal) * high


def outer3(a, b, d):
    full = a[..., :, None, None] * b[..., None, :, None] * d[..., None, None, :]
    return full.reshape(a.shape[:-1] + (-1,))


def draw0():
    ks, kt = mx_kscale(NV), mx_kscale(EO)
    return {
        "x": bf(np.random.uniform(0.02, 0.98, (N, E, J))),
        "cal": bf(np.random.uniform(0.2, 0.8, (E, J))),
        "g": bf(12.0 * np.random.standard_normal((E, NV)) * ks),
        "theta": bf(0.5 * np.random.standard_normal((E, NV, O)) / ks[:, None]),
        "s": bf((1.0 + 0.1 * np.random.standard_normal(EO)) * kt),
        "v": bf(2.0 * np.random.standard_normal((EO, Q)) / np.sqrt(EO) / kt[:, None]),
    }


def core(x, cal, g, theta, s, v):
    x, cal, g, theta, s, v = f64(x), f64(cal), f64(g), f64(theta), f64(s), f64(v)
    n, e, _ = x.shape

    u = calibrate(x, cal)
    p = np.stack([1.0 - u, u], axis=-1)

    p = p.reshape(n, e, TRIPLES, PER, BITS)
    t = outer3(p[:, :, :, 0, :], p[:, :, :, 1, :], p[:, :, :, 2, :])

    w = outer3(t[:, :, 0, :], t[:, :, 1, :], t[:, :, 2, :])

    wg = w * g

    l = mxq(wg.transpose(1, 0, 2), 2, "e4m3") @ mxq(theta, 1, "e4m3")

    h = np.tanh(l)
    flat = h.transpose(1, 0, 2).reshape(n, -1)

    f = flat * s

    return mxq(f, 1, "e4m3") @ mxq(v, 0, "e4m3")


def e4m3fn_bytes(y):
    return np.clip(np.asarray(y, np.float64), -448.0, 448.0).astype(np.float32).astype(ml_dtypes.float8_e4m3fn).view(np.uint8)


def e4m3fn_values(b):
    return np.asarray(b, np.uint8).view(ml_dtypes.float8_e4m3fn).astype(np.float64)


def setup_inputs():
    d = draw0()
    x0 = np.asarray(d['v']).astype(np.float64)
    s = (np.max(np.abs(x0), axis=(1,), keepdims=True) / 448.0).astype(np.float32)
    out = {}
    for k, v in d.items():
        if k == 'v':
            out['v_bytes'] = e4m3fn_bytes(x0 / s.astype(np.float64))
            out['v_scale'] = s
        else:
            out[k] = v
    return out


def reference(x, cal, g, theta, s, v_bytes, v_scale):
    return core(x, cal, g, theta, s, e4m3fn_values(v_bytes) * v_scale.astype(np.float64))

@@ -1,0 +1,495 @@
+from contextlib import ExitStack
+
+import concourse.mybir as mybir
+from concourse.masks import make_identity
+
+F32 = mybir.dt.float32
+BF16 = mybir.dt.bfloat16
+U32 = mybir.dt.uint32
+U8 = mybir.dt.uint8
+FP8 = mybir.dt.float8_e4m3fn
+FP8X4 = mybir.dt.float8_e4m3fn_x4
+ALU = mybir.AluOpType
+ACT = mybir.ActivationFunctionType
+AX = mybir.AxisListType
+
+P = 128
+N, E, J, NV, O, Q = 1024, 4, 9, 512, 512, 512
+T = N // P
+H = T // 2
+PAIRS = T // 2
+STEPS = PAIRS * E
+LAST = E - 1
+FLOPS = 2 * (E * N * NV * O + N * E * O * Q)
+
+
+def tile_calibratedlatticeensemble_kernel(tc, x, cal, g, theta, s, v_bytes, v_scale, out):
+    nc = tc.nc
+    with ExitStack() as ctx:
+        keep = ctx.enter_context(tc.tile_pool(name="keep", bufs=1))
+        work = ctx.enter_context(tc.tile_pool(name="work", bufs=2))
+        ps_s = ctx.enter_context(tc.psum_pool(name="ps_s", bufs=1))
+        ps_g = ctx.enter_context(tc.psum_pool(name="ps_g", bufs=2))
+        ps_l = ctx.enter_context(tc.psum_pool(name="ps_l", bufs=2))
+        ps_m = ctx.enter_context(tc.psum_pool(name="ps_m", bufs=3))
+        ctx.enter_context(tc.manual_schedule())
+
+        xb = keep.tile([P, T * E, J], BF16, name="xb")
+        nc.sync.dma_start(out=xb[:].rearrange("p a j -> p (a j)"), in_=x.rearrange("(c t) e j -> c (t e j)", t=T))
+        calb = keep.tile([P, E * J], BF16, name="calb")
+        nc.sync.dma_start(out=calb[:], in_=cal.rearrange("e j -> (e j)").partition_broadcast(P))
+        gk = keep.tile([P, NV], BF16, name="gk")
+        for e in range(E):
+            nc.sync.dma_start(out=gk[32 * e : 32 * (e + 1), :], in_=g[e].partition_broadcast(32))
+        sp = keep.tile([P, E * 4], BF16, name="sp")
+        vsc = keep.tile([P, E, 4], F32, name="vsc")
+        gp = keep.tile([P, 4], BF16, name="gp")
+        th_raw = []
+        v_raw = []
+        for e in range(E):
+            th_raw.append(keep.tile([P, 4, O], BF16, name=f"th_raw{e}"))
+            v_raw.append(keep.tile([P, 4, Q], U8, name=f"v_raw{e}", align_bytes=64))
+
+        def load_theta(e):
+            nc.sync.dma_start(
+                out=th_raw[e][:].rearrange("p j o -> p (j o)"), in_=theta[e].rearrange("(p j) o -> p (j o)", j=4)
+            )
+
+        def load_v(e):
+            nc.sync.dma_start(
+                out=v_raw[e][:].rearrange("p t q -> p (t q)"),
+                in_=v_bytes[e * O : (e + 1) * O, :].rearrange("(p t) q -> p (t q)", t=4),
+            )
+
+        load_theta(0)
+        nc.scalar.dma_start(out=sp[:].rearrange("p (e t) -> p e t", t=4), in_=s.rearrange("(e p t) -> p e t", p=P, t=4))
+        nc.scalar.dma_start(out=vsc[:], in_=v_scale.rearrange("(e p t) o -> p e (t o)", p=P, t=4))
+        nc.scalar.dma_start(out=gp[:], in_=g[LAST].rearrange("(p t) -> p t", t=4))
+        load_v(0)
+        load_theta(1)
+        load_v(1)
+        load_theta(2)
+        load_v(2)
+        load_theta(3)
+        load_v(3)
+
+        idf = keep.tile([P, P], F32, name="idf")
+        make_identity(nc, idf[:])
+        rr = keep.tile([P, T, P], BF16, name="rr")
+        nc.gpsimd.memset(rr[:], 0.0)
+        idb = keep.tile([P, P], BF16, name="idb")
+        nc.vector.tensor_copy(out=idb[:], in_=idf[:])
+        mask = keep.tile([P, E * 4], F32, name="mask")
+        nc.vector.tensor_reduce(
+            out=mask[:].rearrange("k (e t) -> k e t", t=4),
+            in_=idf[:].rearrange("k (e r t) -> k e t r", r=8, t=4),
+            axis=AX.X,
+            op=ALU.add,
+        )
+
+        cal2 = keep.tile([P, E * J], F32, name="cal2")
+        nc.vector.tensor_scalar(cal2[:], calb[:], 2.0, None, ALU.mult)
+        omc2 = keep.tile([P, E * J], F32, name="omc2")
+        nc.vector.tensor_scalar(omc2[:], calb[:], -2.0, 2.0, ALU.mult, ALU.add)
+        hi = keep.tile([P, T, E * J], F32, name="hi")
+        m1 = keep.tile([P, T, E * J], F32, name="m1")
+        m2 = keep.tile([P, T, E * J], F32, name="m2")
+        pq = keep.tile([P, 2, T * E, J], F32, name="pq")
+        bt = keep.tile([P, T * E, 4], F32, name="bt")
+        rest = keep.tile([P, T * E, 4], F32, name="rest")
+        q01 = keep.tile([P, T * E, 4], F32, name="q01")
+        q23 = keep.tile([P, T * E, 4], F32, name="q23")
+        q45 = keep.tile([P, T * E, 4], F32, name="q45")
+        qa = keep.tile([P, T * E, 16], F32, name="qa")
+        qb = keep.tile([P, T * E, 8], F32, name="qb")
+        xv = xb[:].rearrange("p (t e) j -> p t (e j)", t=T)
+        pqf = pq[:].rearrange("p b a j -> p b (a j)")
+        rv = rr[:].rearrange("p t (e r) -> p (t e) r", r=32)
+        shp = [P, H, E * J]
+        HE = H * E
+
+        calx = keep.tile([P, 2, E * J], F32, name="calx")
+        mn = keep.tile([P, H, E * J], F32, name="mn")
+
+        def calibrate(half, eng):
+            ts = slice(half * H, (half + 1) * H)
+            fs = slice(half * HE * J, (half + 1) * HE * J)
+            c_lo = (cal2[:] if half == 0 else calx[:, 0]).unsqueeze(1).to_broadcast(shp)
+            c_hi = (omc2[:] if half == 0 else calx[:, 1]).unsqueeze(1).to_broadcast(shp)
+            eng.tensor_scalar(hi[:, ts], xv[:, ts], 0.5, 0.5, ALU.max, ALU.subtract)
+            if eng is nc.vector:
+                eng.scalar_tensor_tensor(m1[:, ts], xv[:, ts], 0.5, c_lo, ALU.min, ALU.mult)
+            else:
+                eng.tensor_scalar(mn[:], xv[:, ts], 0.5, 0.0, ALU.min, ALU.add)
+                eng.tensor_tensor(m1[:, ts], mn[:], c_lo, ALU.mult)
+            eng.tensor_tensor(m2[:, ts], hi[:, ts], c_hi, ALU.mult)
+            eng.tensor_tensor(
+                pqf[:, 1, fs],
+                m1[:, ts].rearrange("p t c -> p (t c)"),
+                m2[:, ts].rearrange("p t c -> p (t c)"),
+                ALU.add,
+            )
+            eng.tensor_scalar(pqf[:, 0, fs], pqf[:, 1, fs], -1.0, 1.0, ALU.mult, ALU.add)
+
+        def outer(eng, dst, a, b, na, nb):
+            full = [P, HE, na, nb]
+            eng.tensor_tensor(
+                dst.rearrange("p a (b c) -> p a b c", c=nb),
+                a.unsqueeze(3).to_broadcast(full),
+                b.unsqueeze(2).to_broadcast(full),
+                ALU.mult,
+            )
+
+        def pieces(half, eng):
+            r = slice(half * HE, (half + 1) * HE)
+
+            def fac(j):
+                return pq[:, :, r, j].rearrange("p b a -> p a b")
+
+            outer(eng, bt[:, r], fac(7), fac(8), 2, 2)
+            eng.tensor_copy(out=rv[:, r, 0:4], in_=bt[:, r])
+            eng.tensor_tensor(rest[:, r], bt[:, r], rv[:, r, 0:4], ALU.subtract)
+            eng.tensor_tensor(rv[:, r, 4:8], bt[:, r], rv[:, r, 0:4], ALU.subtract)
+            eng.tensor_tensor(rv[:, r, 8:12], rest[:, r], rv[:, r, 4:8], ALU.subtract)
+
+        def factors(half, eng):
+            r = slice(half * HE, (half + 1) * HE)
+
+            def fac(j):
+                return pq[:, :, r, j].rearrange("p b a -> p a b")
+
+            outer(eng, q01[:, r], fac(0), fac(1), 2, 2)
+            outer(eng, q23[:, r], fac(2), fac(3), 2, 2)
+            outer(eng, q45[:, r], fac(4), fac(5), 2, 2)
+            outer(eng, qa[:, r], q01[:, r], q23[:, r], 4, 4)
+            outer(eng, qb[:, r], q45[:, r], fac(6), 4, 2)
+
+        gw = keep.tile([P, LAST, 4, P], BF16, name="gw")
+        gkv = gk[:].rearrange("k (p t) -> k t p", t=4)
+
+        def make_gw(e):
+            for t in range(4):
+                nc.scalar.activation(
+                    out=gw[:, e, t, :], in_=gkv[:, t, :], func=ACT.Copy, scale=mask[:, 4 * e + t : 4 * e + t + 1]
+                )
+
+        rt = keep.tile([P, T, P], BF16, name="rt")
+
+        def make_rt(half):
+            bank = ps_m.tile([P, 4, P], BF16, name="bank_r", tag="bank_m")
+            for i in range(4):
+                nc.tensor.transpose(bank[:, i, :], rr[:, 4 * half + i, :], idb[:])
+            nc.scalar.copy(out=rt[:, 4 * half : 4 * half + 4, :], in_=bank[:])
+
+        gs = keep.tile([P, 4, T, P], F32, name="gs")
+        gpf = keep.tile([P, 4], F32, name="gpf")
+
+        def make_gs(half, t):
+            bank = ps_m.tile([P, 4, P], F32, name="bank_g", tag="bank_m")
+            for i in range(4):
+                row = (4 * half + i) * E + LAST
+                nc.tensor.transpose(bank[:, i, :], bt[:, row, t : t + 1].to_broadcast([P, P]), idf[:])
+            nc.scalar.activation(
+                out=gs[:, t, 4 * half : 4 * half + 4, :], in_=bank[:], func=ACT.Copy, scale=gpf[:, t : t + 1]
+            )
+
+        aws, ats = {}, {}
+
+        def make_aw(e, half, part, eng):
+            if part == 0:
+                aw = work.tile([P, H, 16, 8], F32, name="aw", bufs=8)
+                aws[e, half] = aw
+            full = [P, 2, 16, 8]
+            rows = slice(half * H + 2 * part, half * H + 2 * part + 2)
+            eng.tensor_tensor(
+                aws[e, half][:, 2 * part : 2 * part + 2],
+                qa[:].rearrange("p (t e) a -> p t e a", e=E)[:, rows, e, :].unsqueeze(3).to_broadcast(full),
+                qb[:].rearrange("p (t e) b -> p t e b", e=E)[:, rows, e, :].unsqueeze(2).to_broadcast(full),
+                ALU.mult,
+            )
+
+        def aw_col(e, tt):
+            return aws[e, tt // H][:, tt % H].rearrange("p a b -> p (a b)")
+
+        def make_at(e, half):
+            bank = ps_m.tile([P, H, P], F32, name="bank_a", tag="bank_m")
+            for i in range(H):
+                nc.tensor.transpose(bank[:, i, :], aw_col(e, half * H + i), idf[:])
+            at = work.tile([P, H, P], F32, name="at", bufs=6)
+            nc.scalar.copy(out=at[:], in_=bank[:])
+            ats[e, half] = at
+
+        th_c, th_s, v_c, v_s = [], [], [], []
+        for e in range(E):
+            th_c.append(keep.tile([P, O], U32, name=f"th_c{e}", align_bytes=64))
+            th_s.append(keep.tile([P, O], U8, name=f"th_s{e}", align_bytes=64))
+            v_c.append(keep.tile([P, Q], U32, name=f"v_c{e}", align_bytes=64))
+            v_s.append(keep.tile([P, Q], U8, name=f"v_s{e}", align_bytes=64))
+
+        def quant(codes, scales, src):
+            nc.vector.quantize_mx(out=codes.bitcast(FP8X4), scales=scales, in_=src)
+
+        th_g, v_w = {}, {}
+
+        def theta_group(e, t):
+            if t == 0:
+                th_gt = work.tile([P, 4, P, 4], BF16, name="th_gt", align_bytes=64)
+                th_g[e] = th_gt
+            nc.scalar.copy(
+                out=th_g[e][:, t], in_=th_raw[e][:].rearrange("p j (m t) -> p t m j", t=4)[:, t]
+            )
+
+        def theta_quant(e):
+            quant(th_c[e][:], th_s[e][:], th_g[e][:].rearrange("p t m j -> p (t m j)"))
+
+        def v_widen(e, t):
+            if t == 0:
+                v_wt = work.tile([P, 4, Q], BF16, name="v_wt")
+                v_w[e] = v_wt
+            nc.scalar.activation(
+                out=v_w[e][:, t, :], in_=v_raw[e][:, t, :].bitcast(FP8), func=ACT.Copy, scale=vsc[:, e, t : t + 1]
+            )
+
+        def v_quant(e):
+            grp = work.tile([P, Q, 4], BF16, name="v_g", align_bytes=64)
+            nc.vector.tensor_copy(out=grp[:], in_=v_w[e][:].rearrange("p t q -> p q t"))
+            return grp
+
+        gbanks, wgs, wq, hs, ffs, fq, accs = {}, {}, {}, {}, {}, {}, {}
+
+        def gains(i):
+            e, pr = divmod(i, PAIRS)
+            if e == LAST:
+                if pr % 2 == 0:
+                    bank_c = ps_g.tile([P, 4, P], F32, name="bank_c", tag="bank_gb")
+                    for j in range(H):
+                        nc.tensor.transpose(bank_c[:, j, :], aw_col(e, 2 * pr + j), idf[:])
+                    for j in range(H):
+                        gbanks[i + j // 2, j % 2] = bank_c
+                return
+            for ti in range(2):
+                bank = ps_g.tile([P, 4, P], F32, name="bank_gb", tag="bank_gb")
+                tt = 2 * pr + ti
+                for t in range(4):
+                    nc.tensor.matmul(bank[:, t, :], lhsT=gw[:, e, t, :], rhs=rt[:, tt, :], start=True, stop=True)
+                gbanks[i, ti] = bank
+
+        def product(i, ti):
+            e, pr = divmod(i, PAIRS)
+            if ti == 0:
+                wg = work.tile([P, 2, P, 4], BF16, name="wg", align_bytes=64, bufs=3)
+                wgs[i] = wg
+            tt = 2 * pr + ti
+            bank = gbanks[i, ti]
+            if e == LAST:
+                gain, corner = gs[:, :, tt, :], bank[:, tt % H, :]
+            else:
+                gain, corner = bank[:], ats[e, tt // H][:, tt % H]
+            nc.vector.tensor_tensor(
+                wgs[i][:, ti],
+                gain.rearrange("p t n -> p n t"),
+                corner.unsqueeze(2).to_broadcast([P, P, 4]),
+                ALU.mult,
+            )
+
+        def quant_w(i, lo=0, n=2):
+            if lo == 0:
+                w_c = work.tile([P, 2 * P], U32, name="w_c", align_bytes=64, bufs=3)
+                w_s = work.tile([P, 2 * P], U8, name="w_s", align_bytes=64, bufs=3)
+                wq[i] = (w_c, w_s)
+            c, sc = wq[i]
+            cols = slice(lo * P, (lo + n) * P)
+            quant(c[:, cols], sc[:, cols], wgs[i][:, lo : lo + n].rearrange("p a n t -> p (a n t)"))
+
+        def lattice(i, ti):
+            e, pr = divmod(i, PAIRS)
+            c, sc = wq[i]
+            if ti == 0:
+                h = work.tile([P, 2, P, 4], F32, name="h", bufs=3)
+                hs[i] = h
+            bank = ps_l.tile([P, 4, P], F32, name="bank_l")
+            cols = slice(ti * P, (ti + 1) * P)
+            for t in range(4):
+                oc = slice(t * P, (t + 1) * P)
+                nc.tensor.matmul_mx(
+                    out=bank[:, t, :],
+                    lhsT=th_c[e][:, oc].bitcast(FP8X4),
+                    lhsT_scale=th_s[e][:, oc],
+                    rhs=c[:, cols].bitcast(FP8X4),
+                    rhs_scale=sc[:, cols],
+                    start=True,
+                    stop=True,
+                )
+            nc.scalar.activation(out=hs[i][:, ti], in_=bank[:].rearrange("p t n -> p n t"), func=ACT.Tanh)
+
+        s_ps = ps_s.tile([P, E * 4], F32, name="s_ps")
+
+        def gain_f(i, ti, eng):
+            e = i // PAIRS
+            if ti == 0:
+                f = work.tile([P, 2, P, 4], BF16, name="f", align_bytes=64, bufs=2)
+                ffs[i] = f
+            src = sp if eng is nc.gpsimd else s_ps
+            eng.tensor_tensor(
+                ffs[i][:, ti],
+                hs[i][:, ti],
+                src[:, 4 * e : 4 * e + 4].unsqueeze(1).to_broadcast([P, P, 4]),
+                ALU.mult,
+            )
+
+        def quant_f(i, lo=0, n=2):
+            if lo == 0:
+                f_c = keep.tile([P, 2 * P], U32, name=f"f_c{i}", align_bytes=64)
+                f_s = keep.tile([P, 2 * P], U8, name=f"f_s{i}", align_bytes=64)
+                fq[i] = (f_c, f_s)
+            c, sc = fq[i]
+            cols = slice(lo * P, (lo + n) * P)
+            quant(c[:, cols], sc[:, cols], ffs[i][:, lo : lo + n].rearrange("p a n t -> p (a n t)"))
+
+        out_v = out.rearrange("(c t) q -> c t q", t=T)
+
+        def mix(tt, e):
+            if e == 0 and tt not in (3, 7):
+                acc = ps_m.tile([P, Q], F32, name="acc", tag="bank_m")
+                accs[tt] = acc
+            elif e == 0:
+                acc_g = ps_g.tile([P, Q], F32, name="acc_g", tag="bank_gb")
+                accs[tt] = acc_g
+            c, sc = fq[e * PAIRS + tt // 2]
+            cols = slice(tt % 2 * P, (tt % 2 + 1) * P)
+            nc.tensor.matmul_mx(
+                out=accs[tt][:],
+                lhsT=c[:, cols].bitcast(FP8X4),
+                lhsT_scale=sc[:, cols],
+                rhs=v_c[e][:].bitcast(FP8X4),
+                rhs_scale=v_s[e][:],
+                start=(e == 0),
+                stop=(e == LAST),
+            )
+
+        def finish(tt, split=False):
+            res = work.tile([P, Q], F32, name="res", bufs=4)
+            if split:
+                half_q = Q // 2
+                nc.scalar.copy(out=res[:, 0:half_q], in_=accs[tt][:, 0:half_q])
+                nc.sync.dma_start(out=out_v[:, tt, 0:half_q], in_=res[:, 0:half_q])
+                nc.vector.tensor_copy(out=res[:, half_q:Q], in_=accs[tt][:, half_q:Q])
+                nc.sync.dma_start(out=out_v[:, tt, half_q:Q], in_=res[:, half_q:Q])
+            else:
+                nc.scalar.copy(out=res[:], in_=accs[tt][:])
+                nc.sync.dma_start(out=out_v[:, tt, :], in_=res[:])
+
+        V, G = nc.vector, nc.gpsimd
+        make_gw(0)
+        calibrate(0, V)
+        factors(0, V)
+        make_aw(0, 0, 0, V)
+        make_aw(0, 0, 1, V)
+        pieces(0, V)
+        nc.vector.tensor_copy(out=calx[:, 0], in_=cal2[:])
+        nc.vector.tensor_copy(out=calx[:, 1], in_=omc2[:])
+        nc.vector.tensor_copy(out=gpf[:], in_=gp[:])
+        calibrate(1, V)
+        pieces(1, G)
+        factors(1, V)
+        make_aw(0, 1, 0, V)
+        make_aw(0, 1, 1, V)
+        for t in range(3):
+            theta_group(0, t)
+        make_at(0, 0)
+        make_rt(0)
+        theta_group(0, 3)
+        gains(0)
+        nc.tensor.matmul(s_ps[:], lhsT=idb[:], rhs=sp[:], start=True, stop=True)
+        make_aw(1, 0, 0, G)
+        make_aw(1, 0, 1, G)
+        for t in range(4):
+            v_widen(0, t)
+        make_rt(1)
+        make_gw(1)
+        theta_quant(0)
+
+        v_g = {}
+
+        def v_pack(e):
+            v_g[e] = v_quant(e)
+
+        def v_codes(e):
+            quant(v_c[e][:], v_s[e][:], v_g[e][:].rearrange("p q t -> p (q t)"))
+
+        def th(e, *ts):
+            for t in ts:
+                theta_group(e, t)
+
+        def vw(e, *ts):
+            for t in ts:
+                v_widen(e, t)
+
+        def gsl(h, *ts):
+            for t in ts:
+                make_gs(h, t)
+
+        def mx3(*tts):
+            for tt in tts:
+                for e2 in range(LAST):
+                    mix(tt, e2)
+
+        def fin(*tts):
+            for tt in tts:
+                mix(tt, LAST)
+                finish(tt)
+
+        extra = {
+            0: lambda: (make_aw(1, 1, 0, G), make_aw(1, 1, 1, G), make_at(0, 1), make_at(1, 0), th(1, 0)),
+            1: lambda: (th(1, 1, 2, 3), v_pack(0)),
+            2: lambda: (make_aw(2, 0, 0, G), make_at(1, 1), make_gw(2), vw(1, 0), v_codes(0)),
+            3: lambda: (make_aw(2, 0, 1, G), vw(1, 1, 2, 3)),
+            4: lambda: (make_aw(2, 1, 0, G), th(2, 0, 1), make_at(2, 0)),
+            5: lambda: (make_aw(2, 1, 1, G), v_pack(1), th(2, 2, 3), make_at(2, 1)),
+            6: lambda: (make_aw(3, 0, 0, G), v_codes(1), vw(2, 0, 1, 2)),
+            7: lambda: (make_aw(3, 0, 1, G), vw(2, 3), gsl(0, 0, 1)),
+            8: lambda: (make_aw(3, 1, 0, G), v_pack(2), th(3, 0, 1), gsl(0, 2)),
+            9: lambda: (make_aw(3, 1, 1, G), v_codes(2), th(3, 2, 3), gsl(0, 3)),
+            10: lambda: (gsl(1, 0, 1), vw(3, 0)),
+            11: lambda: (gsl(1, 2, 3), vw(3, 1)),
+            12: lambda: (vw(3, 2, 3), mx3(0, 1)),
+            13: lambda: (v_pack(3), mx3(2)),
+            14: lambda: (fin(0, 1), mx3(3), fin(2, 3)),
+            15: lambda: (mx3(4, 5, 6), fin(4, 5), mx3(7)),
+        }
+        for k in range(STEPS):
+            last = k == STEPS - 1
+            product(k, 0)
+            if last:
+                quant_w(k, 0, 1)
+                lattice(k, 0)
+            product(k, 1)
+            if not last:
+                gains(k + 1)
+            late = [k - 2] if 2 <= k <= 12 else [11, 12] if k == 13 else [k - 1] if k > 13 else []
+            for i in late:
+                gain_f(i, 0, V)
+                gain_f(i, 1, G)
+            if k == 14:
+                v_codes(3)
+            if k % PAIRS == 0 and k > 0:
+                theta_quant(k // PAIRS)
+            if last:
+                quant_w(k, 1, 1)
+                lattice(k, 1)
+            else:
+                quant_w(k)
+                lattice(k, 0)
+                lattice(k, 1)
+            for i in late:
+                quant_f(i)
+            extra[k]()
+
+        gain_f(STEPS - 1, 0, V)
+        quant_f(STEPS - 1, 0, 1)
+        gain_f(STEPS - 1, 1, V)
+        quant_f(STEPS - 1, 1, 1)
+        mix(6, LAST)
+        finish(6, split=True)
+        mix(7, LAST)
+        finish(7, split=True)

@@ -65,13 +65,10 @@ def tile_calibratedlatticeensemble_kernel(tc, x, cal, g, theta, s, v_bytes, v_sc
         nc.scalar.dma_start(out=sp[:].rearrange("p (e t) -> p e t", t=4), in_=s.rearrange("(e p t) -> p e t", p=P, t=4))
         nc.scalar.dma_start(out=vsc[:], in_=v_scale.rearrange("(e p t) o -> p e (t o)", p=P, t=4))
         nc.scalar.dma_start(out=gp[:], in_=g[LAST].rearrange("(p t) -> p t", t=4))
-        load_v(0)
-        load_theta(1)
-        load_v(1)
-        load_theta(2)
-        load_v(2)
-        load_theta(3)
-        load_v(3)
+        for e in range(1, E):
+            load_theta(e)
+        for e in range(E):
+            load_v(e)
 
         idf = keep.tile([P, P], F32, name="idf")
         make_identity(nc, idf[:])
@@ -108,61 +105,62 @@ def tile_calibratedlatticeensemble_kernel(tc, x, cal, g, theta, s, v_bytes, v_sc
         shp = [P, H, E * J]
         HE = H * E
 
-        calx = keep.tile([P, 2, E * J], F32, name="calx")
-        mn = keep.tile([P, H, E * J], F32, name="mn")
-
-        def calibrate(half, eng):
+        def calibrate(half):
             ts = slice(half * H, (half + 1) * H)
             fs = slice(half * HE * J, (half + 1) * HE * J)
-            c_lo = (cal2[:] if half == 0 else calx[:, 0]).unsqueeze(1).to_broadcast(shp)
-            c_hi = (omc2[:] if half == 0 else calx[:, 1]).unsqueeze(1).to_broadcast(shp)
-            eng.tensor_scalar(hi[:, ts], xv[:, ts], 0.5, 0.5, ALU.max, ALU.subtract)
-            if eng is nc.vector:
-                eng.scalar_tensor_tensor(m1[:, ts], xv[:, ts], 0.5, c_lo, ALU.min, ALU.mult)
-            else:
-                eng.tensor_scalar(mn[:], xv[:, ts], 0.5, 0.0, ALU.min, ALU.add)
-                eng.tensor_tensor(m1[:, ts], mn[:], c_lo, ALU.mult)
-            eng.tensor_tensor(m2[:, ts], hi[:, ts], c_hi, ALU.mult)
-            eng.tensor_tensor(
-                pqf[:, 1, fs],
-                m1[:, ts].rearrange("p t c -> p (t c)"),
-                m2[:, ts].rearrange("p t c -> p (t c)"),
-                ALU.add,
-            )
-            eng.tensor_scalar(pqf[:, 0, fs], pqf[:, 1, fs], -1.0, 1.0, ALU.mult, ALU.add)
+            V = nc.vector
+            return [
+                lambda: V.tensor_scalar(hi[:, ts], xv[:, ts], 0.5, 0.5, ALU.max, ALU.subtract),
+                lambda: V.scalar_tensor_tensor(
+                    m1[:, ts], xv[:, ts], 0.5, cal2[:].unsqueeze(1).to_broadcast(shp), ALU.min, ALU.mult
+                ),
+                lambda: V.tensor_tensor(m2[:, ts], hi[:, ts], omc2[:].unsqueeze(1).to_broadcast(shp), ALU.mult),
+                lambda: V.tensor_tensor(
+                    pqf[:, 1, fs],
+                    m1[:, ts].rearrange("p t c -> p (t c)"),
+                    m2[:, ts].rearrange("p t c -> p (t c)"),
+                    ALU.add,
+                ),
+                lambda: V.tensor_scalar(pqf[:, 0, fs], pqf[:, 1, fs], -1.0, 1.0, ALU.mult, ALU.add),
+            ]
 
-        def outer(eng, dst, a, b, na, nb):
+        def outer(dst, a, b, na, nb):
             full = [P, HE, na, nb]
-            eng.tensor_tensor(
+            nc.vector.tensor_tensor(
                 dst.rearrange("p a (b c) -> p a b c", c=nb),
                 a.unsqueeze(3).to_broadcast(full),
                 b.unsqueeze(2).to_broadcast(full),
                 ALU.mult,
             )
 
-        def pieces(half, eng):
+        def pieces(half):
             r = slice(half * HE, (half + 1) * HE)
 
             def fac(j):
                 return pq[:, :, r, j].rearrange("p b a -> p a b")
 
-            outer(eng, bt[:, r], fac(7), fac(8), 2, 2)
-            eng.tensor_copy(out=rv[:, r, 0:4], in_=bt[:, r])
-            eng.tensor_tensor(rest[:, r], bt[:, r], rv[:, r, 0:4], ALU.subtract)
-            eng.tensor_tensor(rv[:, r, 4:8], bt[:, r], rv[:, r, 0:4], ALU.subtract)
-            eng.tensor_tensor(rv[:, r, 8:12], rest[:, r], rv[:, r, 4:8], ALU.subtract)
+            V = nc.vector
+            return [
+                lambda: outer(bt[:, r], fac(7), fac(8), 2, 2),
+                lambda: V.tensor_copy(out=rv[:, r, 0:4], in_=bt[:, r]),
+                lambda: V.tensor_tensor(rest[:, r], bt[:, r], rv[:, r, 0:4], ALU.subtract),
+                lambda: V.tensor_tensor(rv[:, r, 4:8], bt[:, r], rv[:, r, 0:4], ALU.subtract),
+                lambda: V.tensor_tensor(rv[:, r, 8:12], rest[:, r], rv[:, r, 4:8], ALU.subtract),
+            ]
 
-        def factors(half, eng):
+        def factors(half):
             r = slice(half * HE, (half + 1) * HE)
 
             def fac(j):
                 return pq[:, :, r, j].rearrange("p b a -> p a b")
 
-            outer(eng, q01[:, r], fac(0), fac(1), 2, 2)
-            outer(eng, q23[:, r], fac(2), fac(3), 2, 2)
-            outer(eng, q45[:, r], fac(4), fac(5), 2, 2)
-            outer(eng, qa[:, r], q01[:, r], q23[:, r], 4, 4)
-            outer(eng, qb[:, r], q45[:, r], fac(6), 4, 2)
+            return [
+                lambda: outer(q01[:, r], fac(0), fac(1), 2, 2),
+                lambda: outer(q23[:, r], fac(2), fac(3), 2, 2),
+                lambda: outer(q45[:, r], fac(4), fac(5), 2, 2),
+                lambda: outer(qa[:, r], q01[:, r], q23[:, r], 4, 4),
+                lambda: outer(qb[:, r], q45[:, r], fac(6), 4, 2),
+            ]
 
         gw = keep.tile([P, LAST, 4, P], BF16, name="gw")
         gkv = gk[:].rearrange("k (p t) -> k t p", t=4)
@@ -233,7 +231,7 @@ def tile_calibratedlatticeensemble_kernel(tc, x, cal, g, theta, s, v_bytes, v_sc
 
         def theta_group(e, t):
             if t == 0:
-                th_gt = work.tile([P, 4, P, 4], BF16, name="th_gt", align_bytes=64)
+                th_gt = work.tile([P, 4, P, 4], BF16, name="th_gt", align_bytes=64, bufs=4)
                 th_g[e] = th_gt
             nc.scalar.copy(
                 out=th_g[e][:, t], in_=th_raw[e][:].rearrange("p j (m t) -> p t m j", t=4)[:, t]
@@ -244,23 +242,29 @@ def tile_calibratedlatticeensemble_kernel(tc, x, cal, g, theta, s, v_bytes, v_sc
 
         def v_widen(e, t):
             if t == 0:
-                v_wt = work.tile([P, 4, Q], BF16, name="v_wt")
+                v_wt = work.tile([P, 4, Q], BF16, name="v_wt", bufs=4)
                 v_w[e] = v_wt
             nc.scalar.activation(
                 out=v_w[e][:, t, :], in_=v_raw[e][:, t, :].bitcast(FP8), func=ACT.Copy, scale=vsc[:, e, t : t + 1]
             )
 
         def v_quant(e):
-            grp = work.tile([P, Q, 4], BF16, name="v_g", align_bytes=64)
+            grp = work.tile([P, Q, 4], BF16, name="v_g", align_bytes=64, bufs=4)
             nc.vector.tensor_copy(out=grp[:], in_=v_w[e][:].rearrange("p t q -> p q t"))
             return grp
 
         gbanks, wgs, wq, hs, ffs, fq, accs = {}, {}, {}, {}, {}, {}, {}
 
+        def member(i):
+            return i % 8 // 2
+
+        def pair(i):
+            return 2 * (i // 8) + i % 2
+
         def gains(i):
-            e, pr = divmod(i, PAIRS)
+            e, pr = member(i), pair(i)
             if e == LAST:
-                if pr % 2 == 0:
+                if i % 2 == 0:
                     bank_c = ps_g.tile([P, 4, P], F32, name="bank_c", tag="bank_gb")
                     for j in range(H):
                         nc.tensor.transpose(bank_c[:, j, :], aw_col(e, 2 * pr + j), idf[:])
@@ -275,7 +279,7 @@ def tile_calibratedlatticeensemble_kernel(tc, x, cal, g, theta, s, v_bytes, v_sc
                 gbanks[i, ti] = bank
 
         def product(i, ti):
-            e, pr = divmod(i, PAIRS)
+            e, pr = member(i), pair(i)
             if ti == 0:
                 wg = work.tile([P, 2, P, 4], BF16, name="wg", align_bytes=64, bufs=3)
                 wgs[i] = wg
@@ -302,7 +306,7 @@ def tile_calibratedlatticeensemble_kernel(tc, x, cal, g, theta, s, v_bytes, v_sc
             quant(c[:, cols], sc[:, cols], wgs[i][:, lo : lo + n].rearrange("p a n t -> p (a n t)"))
 
         def lattice(i, ti):
-            e, pr = divmod(i, PAIRS)
+            e, pr = member(i), pair(i)
             c, sc = wq[i]
             if ti == 0:
                 h = work.tile([P, 2, P, 4], F32, name="h", bufs=3)
@@ -325,9 +329,10 @@ def tile_calibratedlatticeensemble_kernel(tc, x, cal, g, theta, s, v_bytes, v_sc
         s_ps = ps_s.tile([P, E * 4], F32, name="s_ps")
 
         def gain_f(i, ti, eng):
-            e = i // PAIRS
+            e = member(i)
             if ti == 0:
-                f = work.tile([P, 2, P, 4], BF16, name="f", align_bytes=64, bufs=2)
+                tail = i >= STEPS - 2
+                f = work.tile([P, 2, P, 4], BF16, name="f", tag=f"f{i}" if tail else "f", align_bytes=64, bufs=1)
                 ffs[i] = f
             src = sp if eng is nc.gpsimd else s_ps
             eng.tensor_tensor(
@@ -349,13 +354,13 @@ def tile_calibratedlatticeensemble_kernel(tc, x, cal, g, theta, s, v_bytes, v_sc
         out_v = out.rearrange("(c t) q -> c t q", t=T)
 
         def mix(tt, e):
-            if e == 0 and tt not in (3, 7):
+            if e == 0 and tt not in (6, 7):
                 acc = ps_m.tile([P, Q], F32, name="acc", tag="bank_m")
                 accs[tt] = acc
             elif e == 0:
                 acc_g = ps_g.tile([P, Q], F32, name="acc_g", tag="bank_gb")
                 accs[tt] = acc_g
-            c, sc = fq[e * PAIRS + tt // 2]
+            c, sc = fq[tt // 4 * 8 + e * 2 + tt // 2 % 2]
             cols = slice(tt % 2 * P, (tt % 2 + 1) * P)
             nc.tensor.matmul_mx(
                 out=accs[tt][:],
@@ -368,7 +373,7 @@ def tile_calibratedlatticeensemble_kernel(tc, x, cal, g, theta, s, v_bytes, v_sc
             )
 
         def finish(tt, split=False):
-            res = work.tile([P, Q], F32, name="res", bufs=4)
+            res = work.tile([P, Q], F32, name="res", bufs=8)
             if split:
                 half_q = Q // 2
                 nc.scalar.copy(out=res[:, 0:half_q], in_=accs[tt][:, 0:half_q])
@@ -380,20 +385,22 @@ def tile_calibratedlatticeensemble_kernel(tc, x, cal, g, theta, s, v_bytes, v_sc
                 nc.sync.dma_start(out=out_v[:, tt, :], in_=res[:])
 
         V, G = nc.vector, nc.gpsimd
+        ca, cb, fa, fb, pa, pb = calibrate(0), calibrate(1), factors(0), factors(1), pieces(0), pieces(1)
         make_gw(0)
-        calibrate(0, V)
-        factors(0, V)
+        for op in (
+            ca[:3] + cb[:1] + ca[3:4] + cb[1:2] + ca[4:5] + cb[2:3]
+            + fa[:1] + pa[:1] + fa[1:3] + pa[1:2] + fa[3:4] + pa[2:4] + fa[4:5] + cb[3:4]
+        ):
+            op()
         make_aw(0, 0, 0, V)
+        pa[4]()
         make_aw(0, 0, 1, V)
-        pieces(0, V)
-        nc.vector.tensor_copy(out=calx[:, 0], in_=cal2[:])
-        nc.vector.tensor_copy(out=calx[:, 1], in_=omc2[:])
+        cb[4]()
         nc.vector.tensor_copy(out=gpf[:], in_=gp[:])
-        calibrate(1, V)
-        pieces(1, G)
-        factors(1, V)
-        make_aw(0, 1, 0, V)
-        make_aw(0, 1, 1, V)
+        make_aw(1, 0, 0, V)
+        make_aw(1, 0, 1, V)
+        for op in pb[:1] + fb[:1] + pb[1:2] + fb[1:3] + pb[2:4] + fb[3:4] + pb[4:] + fb[4:]:
+            op()
         for t in range(3):
             theta_group(0, t)
         make_at(0, 0)
@@ -401,13 +408,10 @@ def tile_calibratedlatticeensemble_kernel(tc, x, cal, g, theta, s, v_bytes, v_sc
         theta_group(0, 3)
         gains(0)
         nc.tensor.matmul(s_ps[:], lhsT=idb[:], rhs=sp[:], start=True, stop=True)
-        make_aw(1, 0, 0, G)
-        make_aw(1, 0, 1, G)
-        for t in range(4):
-            v_widen(0, t)
-        make_rt(1)
+        theta_group(1, 0)
+        theta_group(1, 1)
+        make_at(1, 0)
         make_gw(1)
-        theta_quant(0)
 
         v_g = {}
 
@@ -439,56 +443,75 @@ def tile_calibratedlatticeensemble_kernel(tc, x, cal, g, theta, s, v_bytes, v_sc
                 mix(tt, LAST)
                 finish(tt)
 
-        extra = {
-            0: lambda: (make_aw(1, 1, 0, G), make_aw(1, 1, 1, G), make_at(0, 1), make_at(1, 0), th(1, 0)),
-            1: lambda: (th(1, 1, 2, 3), v_pack(0)),
-            2: lambda: (make_aw(2, 0, 0, G), make_at(1, 1), make_gw(2), vw(1, 0), v_codes(0)),
-            3: lambda: (make_aw(2, 0, 1, G), vw(1, 1, 2, 3)),
-            4: lambda: (make_aw(2, 1, 0, G), th(2, 0, 1), make_at(2, 0)),
-            5: lambda: (make_aw(2, 1, 1, G), v_pack(1), th(2, 2, 3), make_at(2, 1)),
-            6: lambda: (make_aw(3, 0, 0, G), v_codes(1), vw(2, 0, 1, 2)),
-            7: lambda: (make_aw(3, 0, 1, G), vw(2, 3), gsl(0, 0, 1)),
-            8: lambda: (make_aw(3, 1, 0, G), v_pack(2), th(3, 0, 1), gsl(0, 2)),
-            9: lambda: (make_aw(3, 1, 1, G), v_codes(2), th(3, 2, 3), gsl(0, 3)),
-            10: lambda: (gsl(1, 0, 1), vw(3, 0)),
-            11: lambda: (gsl(1, 2, 3), vw(3, 1)),
-            12: lambda: (vw(3, 2, 3), mx3(0, 1)),
-            13: lambda: (v_pack(3), mx3(2)),
-            14: lambda: (fin(0, 1), mx3(3), fin(2, 3)),
-            15: lambda: (mx3(4, 5, 6), fin(4, 5), mx3(7)),
+        def aw(e, half):
+            make_aw(e, half, 0, V)
+            make_aw(e, half, 1, V)
+
+        vector_extra = {
+            0: lambda: aw(2, 0),
+            1: lambda: aw(3, 0),
+            3: lambda: aw(0, 1),
+            5: lambda: aw(1, 1),
+            7: lambda: aw(2, 1),
+            8: lambda: v_pack(0),
+            9: lambda: (v_codes(0), aw(3, 1)),
+            10: lambda: v_pack(1),
+            11: lambda: (v_codes(1), v_pack(2)),
+            12: lambda: (v_codes(2), v_pack(3)),
+            13: lambda: v_codes(3),
         }
-        for k in range(STEPS):
-            last = k == STEPS - 1
+        extra = {
+            0: lambda: (th(1, 2, 3), make_gw(2)),
+            1: lambda: (make_at(2, 0), th(2, 0, 1)),
+            2: lambda: (gsl(0, 0, 1), th(2, 2, 3)),
+            3: lambda: (gsl(0, 2, 3), th(3, 0, 1)),
+            4: lambda: (th(3, 2, 3), vw(0, 0)),
+            5: lambda: (make_at(0, 1), make_rt(1), vw(0, 1)),
+            6: lambda: (vw(0, 2, 3), vw(1, 0)),
+            7: lambda: (make_at(1, 1), vw(1, 1, 2)),
+            8: lambda: (vw(1, 3), vw(2, 0, 1)),
+            9: lambda: (make_at(2, 1), vw(2, 2, 3)),
+            10: lambda: (gsl(1, 0, 1), vw(3, 0, 1)),
+            11: lambda: (gsl(1, 2, 3), vw(3, 2, 3)),
+            12: lambda: mx3(0),
+            13: lambda: (mx3(1, 2), fin(0, 1, 2)),
+            14: lambda: (mx3(3), fin(3), mx3(4, 5)),
+        }
+        for k in range(STEPS - 1):
             product(k, 0)
-            if last:
-                quant_w(k, 0, 1)
-                lattice(k, 0)
             product(k, 1)
-            if not last:
-                gains(k + 1)
-            late = [k - 2] if 2 <= k <= 12 else [11, 12] if k == 13 else [k - 1] if k > 13 else []
-            for i in late:
-                gain_f(i, 0, V)
-                gain_f(i, 1, G)
-            if k == 14:
-                v_codes(3)
-            if k % PAIRS == 0 and k > 0:
-                theta_quant(k // PAIRS)
-            if last:
-                quant_w(k, 1, 1)
-                lattice(k, 1)
-            else:
-                quant_w(k)
-                lattice(k, 0)
-                lattice(k, 1)
-            for i in late:
-                quant_f(i)
+            gains(k + 1)
+            if k >= 2:
+                gain_f(k - 2, 0, V)
+                gain_f(k - 2, 1, V if k == 2 else G)
+            if k % 2 == 0 and k < 8:
+                theta_quant(k // 2)
+            quant_w(k)
+            lattice(k, 0)
+            lattice(k, 1)
+            if k in vector_extra:
+                vector_extra[k]()
+            if k >= 2:
+                quant_f(k - 2)
             extra[k]()
 
-        gain_f(STEPS - 1, 0, V)
-        quant_f(STEPS - 1, 0, 1)
-        gain_f(STEPS - 1, 1, V)
-        quant_f(STEPS - 1, 1, 1)
+        k = STEPS - 1
+        for ti in range(2):
+            product(k, ti)
+            quant_w(k, ti, 1)
+            lattice(k, ti)
+        gain_f(k - 2, 0, V)
+        gain_f(k - 2, 1, V)
+        gain_f(k - 1, 0, V)
+        quant_f(k - 2)
+        mx3(6, 7)
+        gain_f(k - 1, 1, V)
+        gain_f(k, 0, V)
+        quant_f(k - 1)
+        fin(4, 5)
+        gain_f(k, 1, V)
+        quant_f(k, 0, 1)
+        quant_f(k, 1, 1)
         mix(6, LAST)
         finish(6, split=True)
         mix(7, LAST)

@@ -36,11 +36,10 @@ def tile_calibratedlatticeensemble_kernel(tc, x, cal, g, theta, s, v_bytes, v_sc
 
         xb = keep.tile([P, T * E, J], BF16, name="xb")
         nc.sync.dma_start(out=xb[:].rearrange("p a j -> p (a j)"), in_=x.rearrange("(c t) e j -> c (t e j)", t=T))
-        calb = keep.tile([P, E * J], BF16, name="calb")
-        nc.sync.dma_start(out=calb[:], in_=cal.rearrange("e j -> (e j)").partition_broadcast(P))
-        gk = keep.tile([P, NV], BF16, name="gk")
-        for e in range(E):
-            nc.sync.dma_start(out=gk[32 * e : 32 * (e + 1), :], in_=g[e].partition_broadcast(32))
+        cg = keep.tile([P, NV + E * J], BF16, name="cg")
+        nc.vector.memset(cg[:], 0.0)
+        nc.sync.dma_start(out=cg[0:1, NV : NV + E * J], in_=cal.rearrange("(o e) j -> o (e j)", o=1))
+        nc.sync.dma_start(out=cg[0:E, 0:NV], in_=g)
         sp = keep.tile([P, E * 4], BF16, name="sp")
         vsc = keep.tile([P, E, 4], F32, name="vsc")
         gp = keep.tile([P, 4], BF16, name="gp")
@@ -62,11 +61,12 @@ def tile_calibratedlatticeensemble_kernel(tc, x, cal, g, theta, s, v_bytes, v_sc
             )
 
         load_theta(0)
-        nc.scalar.dma_start(out=sp[:].rearrange("p (e t) -> p e t", t=4), in_=s.rearrange("(e p t) -> p e t", p=P, t=4))
-        nc.scalar.dma_start(out=vsc[:], in_=v_scale.rearrange("(e p t) o -> p e (t o)", p=P, t=4))
-        nc.scalar.dma_start(out=gp[:], in_=g[LAST].rearrange("(p t) -> p t", t=4))
-        for e in range(1, E):
-            load_theta(e)
+        load_theta(1)
+        nc.sync.dma_start(out=sp[:].rearrange("p (e t) -> p e t", t=4), in_=s.rearrange("(e p t) -> p e t", p=P, t=4))
+        nc.sync.dma_start(out=gp[:], in_=g[LAST].rearrange("(p t) -> p t", t=4))
+        load_theta(2)
+        load_theta(3)
+        nc.sync.dma_start(out=vsc[:], in_=v_scale.rearrange("(e p t) o -> p e (t o)", p=P, t=4))
         for e in range(E):
             load_v(e)
 
@@ -84,10 +84,19 @@ def tile_calibratedlatticeensemble_kernel(tc, x, cal, g, theta, s, v_bytes, v_sc
             op=ALU.add,
         )
 
+        sel = keep.tile([P, E, 32], BF16, name="sel")
+        nc.vector.tensor_copy(out=sel[:], in_=idb[:, 0:E].unsqueeze(2).to_broadcast([P, E, 32]))
+
+        cal_ps = ps_m.tile([P, E * J], F32, name="cal_ps", tag="bank_m")
+        nc.tensor.matmul(cal_ps[:], lhsT=idb[:, 0:1].to_broadcast([P, P]), rhs=cg[:, NV : NV + E * J], start=True, stop=True)
+        g_ps = ps_m.tile([P, NV], F32, name="g_ps", tag="bank_m")
+        nc.tensor.matmul(g_ps[:], lhsT=sel[:].rearrange("k e r -> k (e r)"), rhs=cg[:, 0:NV], start=True, stop=True)
+        gk = keep.tile([P, NV], BF16, name="gk")
+        nc.scalar.copy(out=gk[:], in_=g_ps[:])
         cal2 = keep.tile([P, E * J], F32, name="cal2")
-        nc.vector.tensor_scalar(cal2[:], calb[:], 2.0, None, ALU.mult)
+        nc.vector.tensor_scalar(cal2[:], cal_ps[:], 2.0, None, ALU.mult)
         omc2 = keep.tile([P, E * J], F32, name="omc2")
-        nc.vector.tensor_scalar(omc2[:], calb[:], -2.0, 2.0, ALU.mult, ALU.add)
+        nc.vector.tensor_scalar(omc2[:], cal_ps[:], -2.0, 2.0, ALU.mult, ALU.add)
         hi = keep.tile([P, T, E * J], F32, name="hi")
         m1 = keep.tile([P, T, E * J], F32, name="m1")
         m2 = keep.tile([P, T, E * J], F32, name="m2")

@@ -242,8 +242,10 @@ def tile_calibratedlatticeensemble_kernel(tc, x, cal, g, theta, s, v_bytes, v_sc
             if t == 0:
                 th_gt = work.tile([P, 4, P, 4], BF16, name="th_gt", align_bytes=64, bufs=4)
                 th_g[e] = th_gt
+            ms = slice(32 * t, 32 * (t + 1))
             nc.scalar.copy(
-                out=th_g[e][:, t], in_=th_raw[e][:].rearrange("p j (m t) -> p t m j", t=4)[:, t]
+                out=th_g[e][:, :, ms, :].rearrange("p t m j -> p m t j"),
+                in_=th_raw[e][:].rearrange("p j (m t) -> p m t j", t=4)[:, ms],
             )
 
         def theta_quant(e):
@@ -259,7 +261,9 @@ def tile_calibratedlatticeensemble_kernel(tc, x, cal, g, theta, s, v_bytes, v_sc
 
         def v_quant(e):
             grp = work.tile([P, Q, 4], BF16, name="v_g", align_bytes=64, bufs=4)
-            nc.vector.tensor_copy(out=grp[:], in_=v_w[e][:].rearrange("p t q -> p q t"))
+            nc.vector.tensor_copy(
+                out=grp[:].rearrange("p (c i) t -> p c t i", i=4), in_=v_w[e][:].rearrange("p t (c i) -> p c t i", i=4)
+            )
             return grp
 
         gbanks, wgs, wq, hs, ffs, fq, accs = {}, {}, {}, {}, {}, {}, {}
@@ -295,15 +299,19 @@ def tile_calibratedlatticeensemble_kernel(tc, x, cal, g, theta, s, v_bytes, v_sc
             tt = 2 * pr + ti
             bank = gbanks[i, ti]
             if e == LAST:
-                gain, corner = gs[:, :, tt, :], bank[:, tt % H, :]
+                nc.vector.tensor_tensor(
+                    wgs[i][:, ti].rearrange("p (c i) t -> p c t i", i=4),
+                    gs[:, :, tt, :].rearrange("p t (c i) -> p c t i", i=4),
+                    bank[:, tt % H, :].rearrange("p (c i) -> p c i", i=4).unsqueeze(2).to_broadcast([P, 32, 4, 4]),
+                    ALU.mult,
+                )
             else:
-                gain, corner = bank[:], ats[e, tt // H][:, tt % H]
-            nc.vector.tensor_tensor(
-                wgs[i][:, ti],
-                gain.rearrange("p t n -> p n t"),
-                corner.unsqueeze(2).to_broadcast([P, P, 4]),
-                ALU.mult,
-            )
+                nc.vector.tensor_tensor(
+                    wgs[i][:, ti],
+                    bank[:].rearrange("p t n -> p n t"),
+                    ats[e, tt // H][:, tt % H].unsqueeze(2).to_broadcast([P, P, 4]),
+                    ALU.mult,
+                )
 
         def quant_w(i, lo=0, n=2):
             if lo == 0:

@@ -14,522 +14,535 @@ ACT = mybir.ActivationFunctionType
 AX = mybir.AxisListType
 
 P = 128
+SLOTS = 4
 N, E, J, NV, O, Q = 1024, 4, 9, 512, 512, 512
-T = N // P
-H = T // 2
-PAIRS = T // 2
-STEPS = PAIRS * E
+TILES = N // P
+HALF = TILES // 2
+GROUP = HALF * E
+PAIR = 2
+STEPS = E * TILES // PAIR
 LAST = E - 1
+SPAN = P // E
+VECTOR_COLS = 120
 FLOPS = 2 * (E * N * NV * O + N * E * O * Q)
 
 
 def tile_calibratedlatticeensemble_kernel(tc, x, cal, g, theta, s, v_bytes, v_scale, out):
     nc = tc.nc
+    vector, scalar, gpsimd, tensor = nc.vector, nc.scalar, nc.gpsimd, nc.tensor
     with ExitStack() as ctx:
         keep = ctx.enter_context(tc.tile_pool(name="keep", bufs=1))
-        work = ctx.enter_context(tc.tile_pool(name="work", bufs=2))
-        ps_s = ctx.enter_context(tc.psum_pool(name="ps_s", bufs=1))
-        ps_g = ctx.enter_context(tc.psum_pool(name="ps_g", bufs=2))
-        ps_l = ctx.enter_context(tc.psum_pool(name="ps_l", bufs=2))
-        ps_m = ctx.enter_context(tc.psum_pool(name="ps_m", bufs=3))
+        work = ctx.enter_context(tc.tile_pool(name="work", bufs=3))
+        psum_s = ctx.enter_context(tc.psum_pool(name="psum_s", bufs=1))
+        psum_gain = ctx.enter_context(tc.psum_pool(name="psum_gain", bufs=2))
+        psum_lattice = ctx.enter_context(tc.psum_pool(name="psum_lattice", bufs=2))
+        psum_mixed = ctx.enter_context(tc.psum_pool(name="psum_mixed", bufs=3))
         ctx.enter_context(tc.manual_schedule())
 
-        xb = keep.tile([P, T * E, J], BF16, name="xb")
-        nc.sync.dma_start(out=xb[:].rearrange("p a j -> p (a j)"), in_=x.rearrange("(c t) e j -> c (t e j)", t=T))
-        cg = keep.tile([P, NV + E * J], BF16, name="cg")
-        nc.vector.memset(cg[:], 0.0)
-        nc.sync.dma_start(out=cg[0:1, NV : NV + E * J], in_=cal.rearrange("(o e) j -> o (e j)", o=1))
-        nc.sync.dma_start(out=cg[0:E, 0:NV], in_=g)
-        sp = keep.tile([P, E * 4], BF16, name="sp")
-        vsc = keep.tile([P, E, 4], F32, name="vsc")
-        gp = keep.tile([P, 4], BF16, name="gp")
-        th_raw = []
-        v_raw = []
+        x_sb = keep.tile([P, TILES * E, J], BF16, name="x_sb")
+        nc.sync.dma_start(
+            out=x_sb[:].rearrange("p a j -> p (a j)"), in_=x.rearrange("(c r) e j -> c (r e j)", r=TILES)
+        )
+        rows_sb = keep.tile([P, NV + E * J], BF16, name="rows_sb")
+        vector.memset(rows_sb[:], 0.0)
+        nc.sync.dma_start(out=rows_sb[0:1, NV : NV + E * J], in_=cal.rearrange("(o e) j -> o (e j)", o=1))
+        nc.sync.dma_start(out=rows_sb[0:E, 0:NV], in_=g)
+        s_sb = keep.tile([P, E * SLOTS], BF16, name="s_sb")
+        v_scale_sb = keep.tile([P, E, SLOTS], F32, name="v_scale_sb")
+        g_last_sb = keep.tile([P, SLOTS], BF16, name="g_last_sb")
+        theta_sb, v_bytes_sb = [], []
         for e in range(E):
-            th_raw.append(keep.tile([P, 4, O], BF16, name=f"th_raw{e}"))
-            v_raw.append(keep.tile([P, 4, Q], U8, name=f"v_raw{e}", align_bytes=64))
+            theta_sb.append(keep.tile([P, SLOTS, O], BF16, name=f"theta_sb{e}"))
+            v_bytes_sb.append(keep.tile([P, SLOTS, Q], U8, name=f"v_bytes_sb{e}", align_bytes=64))
 
         def load_theta(e):
             nc.sync.dma_start(
-                out=th_raw[e][:].rearrange("p j o -> p (j o)"), in_=theta[e].rearrange("(p j) o -> p (j o)", j=4)
-            )
-
-        def load_v(e):
-            nc.sync.dma_start(
-                out=v_raw[e][:].rearrange("p t q -> p (t q)"),
-                in_=v_bytes[e * O : (e + 1) * O, :].rearrange("(p t) q -> p (t q)", t=4),
+                out=theta_sb[e][:].rearrange("p j o -> p (j o)"),
+                in_=theta[e].rearrange("(p j) o -> p (j o)", j=SLOTS),
             )
 
         load_theta(0)
         load_theta(1)
-        nc.sync.dma_start(out=sp[:].rearrange("p (e t) -> p e t", t=4), in_=s.rearrange("(e p t) -> p e t", p=P, t=4))
-        nc.sync.dma_start(out=gp[:], in_=g[LAST].rearrange("(p t) -> p t", t=4))
+        nc.sync.dma_start(
+            out=s_sb[:].rearrange("p (e t) -> p e t", t=SLOTS), in_=s.rearrange("(e p t) -> p e t", p=P, t=SLOTS)
+        )
+        nc.sync.dma_start(out=g_last_sb[:], in_=g[LAST].rearrange("(p t) -> p t", t=SLOTS))
         load_theta(2)
         load_theta(3)
-        nc.sync.dma_start(out=vsc[:], in_=v_scale.rearrange("(e p t) o -> p e (t o)", p=P, t=4))
+        nc.sync.dma_start(out=v_scale_sb[:], in_=v_scale.rearrange("(e p t) o -> p e (t o)", p=P, t=SLOTS))
         for e in range(E):
-            load_v(e)
+            nc.sync.dma_start(
+                out=v_bytes_sb[e][:].rearrange("p t q -> p (t q)"),
+                in_=v_bytes[e * O : (e + 1) * O, :].rearrange("(p t) q -> p (t q)", t=SLOTS),
+            )
 
-        idf = keep.tile([P, P], F32, name="idf")
-        make_identity(nc, idf[:])
-        rr = keep.tile([P, T, P], BF16, name="rr")
-        nc.gpsimd.memset(rr[:], 0.0)
-        idb = keep.tile([P, P], BF16, name="idb")
-        nc.vector.tensor_copy(out=idb[:], in_=idf[:])
-        mask = keep.tile([P, E * 4], F32, name="mask")
-        nc.vector.tensor_reduce(
-            out=mask[:].rearrange("k (e t) -> k e t", t=4),
-            in_=idf[:].rearrange("k (e r t) -> k e t r", r=8, t=4),
+        ident_f32 = keep.tile([P, P], F32, name="ident_f32")
+        make_identity(nc, ident_f32[:])
+        pieces = keep.tile([P, TILES, P], BF16, name="pieces")
+        gpsimd.memset(pieces[:], 0.0)
+        ident = keep.tile([P, P], BF16, name="ident")
+        vector.tensor_copy(out=ident[:], in_=ident_f32[:])
+        row_mask = keep.tile([P, E * SLOTS], F32, name="row_mask")
+        vector.tensor_reduce(
+            out=row_mask[:].rearrange("k (e t) -> k e t", t=SLOTS),
+            in_=ident_f32[:].rearrange("k (e d t) -> k e t d", e=E, t=SLOTS),
             axis=AX.X,
             op=ALU.add,
         )
+        spread = keep.tile([P, E, SPAN], BF16, name="spread")
+        vector.tensor_copy(out=spread[:], in_=ident[:, 0:E].unsqueeze(2).to_broadcast([P, E, SPAN]))
 
-        sel = keep.tile([P, E, 32], BF16, name="sel")
-        nc.vector.tensor_copy(out=sel[:], in_=idb[:, 0:E].unsqueeze(2).to_broadcast([P, E, 32]))
+        cal_bank = psum_mixed.tile([P, E * J], F32, name="cal_bank", tag="bank")
+        tensor.matmul(
+            cal_bank[:],
+            lhsT=ident[:, 0:1].to_broadcast([P, P]),
+            rhs=rows_sb[:, NV : NV + E * J],
+            start=True,
+            stop=True,
+        )
+        g_bank = psum_mixed.tile([P, NV], F32, name="g_bank", tag="bank")
+        tensor.matmul(
+            g_bank[:], lhsT=spread[:].rearrange("k e d -> k (e d)"), rhs=rows_sb[:, 0:NV], start=True, stop=True
+        )
+        g_rows = keep.tile([P, SLOTS, P], BF16, name="g_rows")
+        scalar.copy(out=g_rows[:], in_=g_bank[:].rearrange("k (p t) -> k t p", t=SLOTS))
 
-        cal_ps = ps_m.tile([P, E * J], F32, name="cal_ps", tag="bank_m")
-        nc.tensor.matmul(cal_ps[:], lhsT=idb[:, 0:1].to_broadcast([P, P]), rhs=cg[:, NV : NV + E * J], start=True, stop=True)
-        g_ps = ps_m.tile([P, NV], F32, name="g_ps", tag="bank_m")
-        nc.tensor.matmul(g_ps[:], lhsT=sel[:].rearrange("k e r -> k (e r)"), rhs=cg[:, 0:NV], start=True, stop=True)
-        gk = keep.tile([P, NV], BF16, name="gk")
-        nc.scalar.copy(out=gk[:], in_=g_ps[:])
-        cal2 = keep.tile([P, E * J], F32, name="cal2")
-        nc.vector.tensor_scalar(cal2[:], cal_ps[:], 2.0, None, ALU.mult)
-        omc2 = keep.tile([P, E * J], F32, name="omc2")
-        nc.vector.tensor_scalar(omc2[:], cal_ps[:], -2.0, 2.0, ALU.mult, ALU.add)
-        hi = keep.tile([P, T, E * J], F32, name="hi")
-        m1 = keep.tile([P, T, E * J], F32, name="m1")
-        m2 = keep.tile([P, T, E * J], F32, name="m2")
-        pq = keep.tile([P, 2, T * E, J], F32, name="pq")
-        bt = keep.tile([P, T * E, 4], F32, name="bt")
-        rest = keep.tile([P, T * E, 4], F32, name="rest")
-        q01 = keep.tile([P, T * E, 4], F32, name="q01")
-        q23 = keep.tile([P, T * E, 4], F32, name="q23")
-        q45 = keep.tile([P, T * E, 4], F32, name="q45")
-        qa = keep.tile([P, T * E, 16], F32, name="qa")
-        qb = keep.tile([P, T * E, 8], F32, name="qb")
-        xv = xb[:].rearrange("p (t e) j -> p t (e j)", t=T)
-        pqf = pq[:].rearrange("p b a j -> p b (a j)")
-        rv = rr[:].rearrange("p t (e r) -> p (t e) r", r=32)
-        shp = [P, H, E * J]
-        HE = H * E
+        cal_low = keep.tile([P, E * J], F32, name="cal_low")
+        cal_high = keep.tile([P, E * J], F32, name="cal_high")
+        above = keep.tile([P, TILES, E * J], F32, name="above")
+        part_low = keep.tile([P, TILES, E * J], F32, name="part_low")
+        part_high = keep.tile([P, TILES, E * J], F32, name="part_high")
+        factor = keep.tile([P, 2, TILES * E, J], F32, name="factor")
+        low = keep.tile([P, TILES * E, 4], F32, name="low")
+        remainder = keep.tile([P, TILES * E, 4], F32, name="remainder")
+        bits01 = keep.tile([P, TILES * E, 4], F32, name="bits01")
+        bits23 = keep.tile([P, TILES * E, 4], F32, name="bits23")
+        bits45 = keep.tile([P, TILES * E, 4], F32, name="bits45")
+        bits0123 = keep.tile([P, TILES * E, 16], F32, name="bits0123")
+        bits456 = keep.tile([P, TILES * E, 8], F32, name="bits456")
+        x_rows = x_sb[:].rearrange("p (r e) j -> p r (e j)", r=TILES)
+        factor_flat = factor[:].rearrange("p b a j -> p b (a j)")
+        piece = pieces[:].rearrange("p r (e k) -> p (r e) k", k=SPAN)
 
-        def calibrate(half):
-            ts = slice(half * H, (half + 1) * H)
-            fs = slice(half * HE * J, (half + 1) * HE * J)
-            V = nc.vector
+        def calibration(half):
+            ts = slice(half * HALF, (half + 1) * HALF)
+            fs = slice(half * GROUP * J, (half + 1) * GROUP * J)
+            full = [P, HALF, E * J]
             return [
-                lambda: V.tensor_scalar(hi[:, ts], xv[:, ts], 0.5, 0.5, ALU.max, ALU.subtract),
-                lambda: V.scalar_tensor_tensor(
-                    m1[:, ts], xv[:, ts], 0.5, cal2[:].unsqueeze(1).to_broadcast(shp), ALU.min, ALU.mult
+                lambda: vector.tensor_scalar(above[:, ts], x_rows[:, ts], 0.5, 0.5, ALU.max, ALU.subtract),
+                lambda: vector.scalar_tensor_tensor(
+                    part_low[:, ts], x_rows[:, ts], 0.5, cal_low[:].unsqueeze(1).to_broadcast(full), ALU.min, ALU.mult
                 ),
-                lambda: V.tensor_tensor(m2[:, ts], hi[:, ts], omc2[:].unsqueeze(1).to_broadcast(shp), ALU.mult),
-                lambda: V.tensor_tensor(
-                    pqf[:, 1, fs],
-                    m1[:, ts].rearrange("p t c -> p (t c)"),
-                    m2[:, ts].rearrange("p t c -> p (t c)"),
+                lambda: vector.tensor_tensor(
+                    part_high[:, ts], above[:, ts], cal_high[:].unsqueeze(1).to_broadcast(full), ALU.mult
+                ),
+                lambda: vector.tensor_tensor(
+                    factor_flat[:, 1, fs],
+                    part_low[:, ts].rearrange("p r c -> p (r c)"),
+                    part_high[:, ts].rearrange("p r c -> p (r c)"),
                     ALU.add,
                 ),
-                lambda: V.tensor_scalar(pqf[:, 0, fs], pqf[:, 1, fs], -1.0, 1.0, ALU.mult, ALU.add),
+                lambda: vector.tensor_scalar(
+                    factor_flat[:, 0, fs], factor_flat[:, 1, fs], -1.0, 1.0, ALU.mult, ALU.add
+                ),
             ]
 
         def outer(dst, a, b, na, nb):
-            full = [P, HE, na, nb]
-            nc.vector.tensor_tensor(
-                dst.rearrange("p a (b c) -> p a b c", c=nb),
+            full = [P, GROUP, na, nb]
+            vector.tensor_tensor(
+                dst.rearrange("p g (a b) -> p g a b", b=nb),
                 a.unsqueeze(3).to_broadcast(full),
                 b.unsqueeze(2).to_broadcast(full),
                 ALU.mult,
             )
 
-        def pieces(half):
-            r = slice(half * HE, (half + 1) * HE)
+        def bit_pair(half, j):
+            return factor[:, :, half * GROUP : (half + 1) * GROUP, j].rearrange("p b a -> p a b")
 
-            def fac(j):
-                return pq[:, :, r, j].rearrange("p b a -> p a b")
-
-            V = nc.vector
+        def low_weights(half):
+            rs = slice(half * GROUP, (half + 1) * GROUP)
             return [
-                lambda: outer(bt[:, r], fac(7), fac(8), 2, 2),
-                lambda: V.tensor_copy(out=rv[:, r, 0:4], in_=bt[:, r]),
-                lambda: V.tensor_tensor(rest[:, r], bt[:, r], rv[:, r, 0:4], ALU.subtract),
-                lambda: V.tensor_tensor(rv[:, r, 4:8], bt[:, r], rv[:, r, 0:4], ALU.subtract),
-                lambda: V.tensor_tensor(rv[:, r, 8:12], rest[:, r], rv[:, r, 4:8], ALU.subtract),
+                lambda: outer(low[:, rs], bit_pair(half, 7), bit_pair(half, 8), 2, 2),
+                lambda: vector.tensor_copy(out=piece[:, rs, 0:4], in_=low[:, rs]),
+                lambda: vector.tensor_tensor(remainder[:, rs], low[:, rs], piece[:, rs, 0:4], ALU.subtract),
+                lambda: vector.tensor_tensor(piece[:, rs, 4:8], low[:, rs], piece[:, rs, 0:4], ALU.subtract),
+                lambda: vector.tensor_tensor(piece[:, rs, 8:12], remainder[:, rs], piece[:, rs, 4:8], ALU.subtract),
             ]
 
-        def factors(half):
-            r = slice(half * HE, (half + 1) * HE)
-
-            def fac(j):
-                return pq[:, :, r, j].rearrange("p b a -> p a b")
-
+        def high_factors(half):
+            rs = slice(half * GROUP, (half + 1) * GROUP)
             return [
-                lambda: outer(q01[:, r], fac(0), fac(1), 2, 2),
-                lambda: outer(q23[:, r], fac(2), fac(3), 2, 2),
-                lambda: outer(q45[:, r], fac(4), fac(5), 2, 2),
-                lambda: outer(qa[:, r], q01[:, r], q23[:, r], 4, 4),
-                lambda: outer(qb[:, r], q45[:, r], fac(6), 4, 2),
+                lambda: outer(bits01[:, rs], bit_pair(half, 0), bit_pair(half, 1), 2, 2),
+                lambda: outer(bits23[:, rs], bit_pair(half, 2), bit_pair(half, 3), 2, 2),
+                lambda: outer(bits45[:, rs], bit_pair(half, 4), bit_pair(half, 5), 2, 2),
+                lambda: outer(bits0123[:, rs], bits01[:, rs], bits23[:, rs], 4, 4),
+                lambda: outer(bits456[:, rs], bits45[:, rs], bit_pair(half, 6), 4, 2),
             ]
 
-        gw = keep.tile([P, LAST, 4, P], BF16, name="gw")
-        gkv = gk[:].rearrange("k (p t) -> k t p", t=4)
+        g_weight = keep.tile([P, LAST, SLOTS, P], BF16, name="g_weight")
 
-        def make_gw(e):
-            for t in range(4):
-                nc.scalar.activation(
-                    out=gw[:, e, t, :], in_=gkv[:, t, :], func=ACT.Copy, scale=mask[:, 4 * e + t : 4 * e + t + 1]
+        def make_g_weight(e):
+            for t in range(SLOTS):
+                scalar.activation(
+                    out=g_weight[:, e, t, :],
+                    in_=g_rows[:, t, :],
+                    func=ACT.Copy,
+                    scale=row_mask[:, SLOTS * e + t : SLOTS * e + t + 1],
                 )
 
-        rt = keep.tile([P, T, P], BF16, name="rt")
+        pieces_k = keep.tile([P, TILES, P], BF16, name="pieces_k")
 
-        def make_rt(half):
-            bank = ps_m.tile([P, 4, P], BF16, name="bank_r", tag="bank_m")
-            for i in range(4):
-                nc.tensor.transpose(bank[:, i, :], rr[:, 4 * half + i, :], idb[:])
-            nc.scalar.copy(out=rt[:, 4 * half : 4 * half + 4, :], in_=bank[:])
+        def make_pieces_k(half):
+            bank = psum_mixed.tile([P, HALF, P], BF16, name="piece_bank", tag="bank")
+            for i in range(HALF):
+                tensor.transpose(bank[:, i, :], pieces[:, HALF * half + i, :], ident[:])
+            scalar.copy(out=pieces_k[:, HALF * half : HALF * (half + 1), :], in_=bank[:])
 
-        gs = keep.tile([P, 4, T, P], F32, name="gs")
-        gpf = keep.tile([P, 4], F32, name="gpf")
+        gained_last = keep.tile([P, SLOTS, TILES, P], F32, name="gained_last")
+        g_last = keep.tile([P, SLOTS], F32, name="g_last")
 
-        def make_gs(half, t):
-            bank = ps_m.tile([P, 4, P], F32, name="bank_g", tag="bank_m")
-            for i in range(4):
-                row = (4 * half + i) * E + LAST
-                nc.tensor.transpose(bank[:, i, :], bt[:, row, t : t + 1].to_broadcast([P, P]), idf[:])
-            nc.scalar.activation(
-                out=gs[:, t, 4 * half : 4 * half + 4, :], in_=bank[:], func=ACT.Copy, scale=gpf[:, t : t + 1]
-            )
+        def make_gained_last(half, *slots):
+            for t in slots:
+                bank = psum_mixed.tile([P, HALF, P], F32, name="low_bank", tag="bank")
+                for i in range(HALF):
+                    row = (HALF * half + i) * E + LAST
+                    tensor.transpose(bank[:, i, :], low[:, row, t : t + 1].to_broadcast([P, P]), ident_f32[:])
+                scalar.activation(
+                    out=gained_last[:, t, HALF * half : HALF * (half + 1), :],
+                    in_=bank[:],
+                    func=ACT.Copy,
+                    scale=g_last[:, t : t + 1],
+                )
 
-        aws, ats = {}, {}
+        high_rows, high_p = {}, {}
 
-        def make_aw(e, half, part, eng):
+        def make_high(e, half, part):
             if part == 0:
-                aw = work.tile([P, H, 16, 8], F32, name="aw", bufs=8)
-                aws[e, half] = aw
-            full = [P, 2, 16, 8]
-            rows = slice(half * H + 2 * part, half * H + 2 * part + 2)
-            eng.tensor_tensor(
-                aws[e, half][:, 2 * part : 2 * part + 2],
-                qa[:].rearrange("p (t e) a -> p t e a", e=E)[:, rows, e, :].unsqueeze(3).to_broadcast(full),
-                qb[:].rearrange("p (t e) b -> p t e b", e=E)[:, rows, e, :].unsqueeze(2).to_broadcast(full),
+                high_tile = keep.tile([P, HALF, 16, 8], F32, name=f"high_{e}_{half}")
+                high_rows[e, half] = high_tile
+            full = [P, PAIR, 16, 8]
+            rs = slice(half * HALF + PAIR * part, half * HALF + PAIR * (part + 1))
+            vector.tensor_tensor(
+                high_rows[e, half][:, PAIR * part : PAIR * (part + 1)],
+                bits0123[:].rearrange("p (r e) a -> p r e a", e=E)[:, rs, e, :].unsqueeze(3).to_broadcast(full),
+                bits456[:].rearrange("p (r e) b -> p r e b", e=E)[:, rs, e, :].unsqueeze(2).to_broadcast(full),
                 ALU.mult,
             )
 
-        def aw_col(e, tt):
-            return aws[e, tt // H][:, tt % H].rearrange("p a b -> p (a b)")
+        def high_of(e, r):
+            return high_rows[e, r // HALF][:, r % HALF].rearrange("p a b -> p (a b)")
 
-        def make_at(e, half):
-            bank = ps_m.tile([P, H, P], F32, name="bank_a", tag="bank_m")
-            for i in range(H):
-                nc.tensor.transpose(bank[:, i, :], aw_col(e, half * H + i), idf[:])
-            at = work.tile([P, H, P], F32, name="at", bufs=6)
-            nc.scalar.copy(out=at[:], in_=bank[:])
-            ats[e, half] = at
+        def make_high_p(e, half):
+            bank = psum_mixed.tile([P, HALF, P], F32, name="high_bank", tag="bank")
+            for i in range(HALF):
+                tensor.transpose(bank[:, i, :], high_of(e, half * HALF + i), ident_f32[:])
+            high_p_tile = keep.tile([P, HALF, P], F32, name=f"high_p_{e}_{half}")
+            scalar.copy(out=high_p_tile[:], in_=bank[:])
+            high_p[e, half] = high_p_tile
 
-        th_c, th_s, v_c, v_s = [], [], [], []
+        def quantize(codes, scales, src):
+            vector.quantize_mx(out=codes.bitcast(FP8X4), scales=scales, in_=src)
+
+        theta_codes, theta_scales, theta_grouped = [], [], []
+        v_codes, v_scales, v_wide, v_grouped = [], [], [], []
         for e in range(E):
-            th_c.append(keep.tile([P, O], U32, name=f"th_c{e}", align_bytes=64))
-            th_s.append(keep.tile([P, O], U8, name=f"th_s{e}", align_bytes=64))
-            v_c.append(keep.tile([P, Q], U32, name=f"v_c{e}", align_bytes=64))
-            v_s.append(keep.tile([P, Q], U8, name=f"v_s{e}", align_bytes=64))
+            theta_codes.append(keep.tile([P, O], U32, name=f"theta_codes{e}", align_bytes=64))
+            theta_scales.append(keep.tile([P, O], U8, name=f"theta_scales{e}", align_bytes=64))
+            theta_grouped.append(keep.tile([P, SLOTS, P, SLOTS], BF16, name=f"theta_grouped{e}", align_bytes=64))
+            v_codes.append(keep.tile([P, Q], U32, name=f"v_codes{e}", align_bytes=64))
+            v_scales.append(keep.tile([P, Q], U8, name=f"v_scales{e}", align_bytes=64))
+            v_wide.append(keep.tile([P, SLOTS, Q], BF16, name=f"v_wide{e}"))
+            v_grouped.append(keep.tile([P, Q, SLOTS], BF16, name=f"v_grouped{e}", align_bytes=64))
 
-        def quant(codes, scales, src):
-            nc.vector.quantize_mx(out=codes.bitcast(FP8X4), scales=scales, in_=src)
+        def group_theta(e, *quarters, copy=scalar.copy):
+            for i in quarters:
+                ms = slice(P // 4 * i, P // 4 * (i + 1))
+                copy(
+                    out=theta_grouped[e][:, :, ms, :].rearrange("p t m j -> p m t j"),
+                    in_=theta_sb[e][:].rearrange("p j (m t) -> p m t j", t=SLOTS)[:, ms],
+                )
 
-        th_g, v_w = {}, {}
+        def quantize_theta(e):
+            quantize(theta_codes[e][:], theta_scales[e][:], theta_grouped[e][:].rearrange("p t m j -> p (t m j)"))
 
-        def theta_group(e, t):
-            if t == 0:
-                th_gt = work.tile([P, 4, P, 4], BF16, name="th_gt", align_bytes=64, bufs=4)
-                th_g[e] = th_gt
-            ms = slice(32 * t, 32 * (t + 1))
-            nc.scalar.copy(
-                out=th_g[e][:, :, ms, :].rearrange("p t m j -> p m t j"),
-                in_=th_raw[e][:].rearrange("p j (m t) -> p m t j", t=4)[:, ms],
+        def widen_v(e, *slots):
+            for t in slots:
+                scalar.activation(
+                    out=v_wide[e][:, t, :],
+                    in_=v_bytes_sb[e][:, t, :].bitcast(FP8),
+                    func=ACT.Copy,
+                    scale=v_scale_sb[:, e, t : t + 1],
+                )
+
+        def group_v(e, first, end, copy=vector.tensor_copy):
+            copy(
+                out=v_grouped[e][:, first:end].rearrange("p (c i) t -> p c t i", i=4),
+                in_=v_wide[e][:, :, first:end].rearrange("p t (c i) -> p c t i", i=4),
             )
 
-        def theta_quant(e):
-            quant(th_c[e][:], th_s[e][:], th_g[e][:].rearrange("p t m j -> p (t m j)"))
+        def quantize_v(e):
+            quantize(v_codes[e][:], v_scales[e][:], v_grouped[e][:].rearrange("p q t -> p (q t)"))
 
-        def v_widen(e, t):
-            if t == 0:
-                v_wt = work.tile([P, 4, Q], BF16, name="v_wt", bufs=4)
-                v_w[e] = v_wt
-            nc.scalar.activation(
-                out=v_w[e][:, t, :], in_=v_raw[e][:, t, :].bitcast(FP8), func=ACT.Copy, scale=vsc[:, e, t : t + 1]
-            )
-
-        def v_quant(e):
-            grp = work.tile([P, Q, 4], BF16, name="v_g", align_bytes=64, bufs=4)
-            nc.vector.tensor_copy(
-                out=grp[:].rearrange("p (c i) t -> p c t i", i=4), in_=v_w[e][:].rearrange("p t (c i) -> p c t i", i=4)
-            )
-            return grp
-
-        gbanks, wgs, wq, hs, ffs, fq, accs = {}, {}, {}, {}, {}, {}, {}
+        gain_banks, weights, weight_codes, tanhs, channels, channel_codes, sums = {}, {}, {}, {}, {}, {}, {}
 
         def member(i):
-            return i % 8 // 2
+            return i % (STEPS // 2) // 2
 
-        def pair(i):
-            return 2 * (i // 8) + i % 2
+        def row_tile(i, side):
+            return i // (STEPS // 2) * HALF + i % 2 * PAIR + side
+
+        def step_of(r, e):
+            return r // HALF * (STEPS // 2) + e * 2 + r // PAIR % 2
 
         def gains(i):
-            e, pr = member(i), pair(i)
-            if e == LAST:
-                if i % 2 == 0:
-                    bank_c = ps_g.tile([P, 4, P], F32, name="bank_c", tag="bank_gb")
-                    for j in range(H):
-                        nc.tensor.transpose(bank_c[:, j, :], aw_col(e, 2 * pr + j), idf[:])
-                    for j in range(H):
-                        gbanks[i + j // 2, j % 2] = bank_c
-                return
-            for ti in range(2):
-                bank = ps_g.tile([P, 4, P], F32, name="bank_gb", tag="bank_gb")
-                tt = 2 * pr + ti
-                for t in range(4):
-                    nc.tensor.matmul(bank[:, t, :], lhsT=gw[:, e, t, :], rhs=rt[:, tt, :], start=True, stop=True)
-                gbanks[i, ti] = bank
+            e = member(i)
+            if e < LAST:
+                for side in range(PAIR):
+                    gain_bank = psum_gain.tile([P, SLOTS, P], F32, name="gain_bank", tag="bank")
+                    for t in range(SLOTS):
+                        tensor.matmul(
+                            gain_bank[:, t, :],
+                            lhsT=g_weight[:, e, t, :],
+                            rhs=pieces_k[:, row_tile(i, side), :],
+                            start=True,
+                            stop=True,
+                        )
+                    gain_banks[i, side] = gain_bank
+            elif i % 2 == 0:
+                last_bank = psum_gain.tile([P, HALF, P], F32, name="last_bank", tag="bank")
+                for j in range(HALF):
+                    tensor.transpose(last_bank[:, j, :], high_of(e, row_tile(i, j)), ident_f32[:])
+                    gain_banks[i + j // PAIR, j % PAIR] = last_bank
 
-        def product(i, ti):
-            e, pr = member(i), pair(i)
-            if ti == 0:
-                wg = work.tile([P, 2, P, 4], BF16, name="wg", align_bytes=64, bufs=3)
-                wgs[i] = wg
-            tt = 2 * pr + ti
-            bank = gbanks[i, ti]
-            if e == LAST:
-                nc.vector.tensor_tensor(
-                    wgs[i][:, ti].rearrange("p (c i) t -> p c t i", i=4),
-                    gs[:, :, tt, :].rearrange("p t (c i) -> p c t i", i=4),
-                    bank[:, tt % H, :].rearrange("p (c i) -> p c i", i=4).unsqueeze(2).to_broadcast([P, 32, 4, 4]),
+        def product(i, side):
+            e, r = member(i), row_tile(i, side)
+            if side == 0:
+                weight = work.tile([P, PAIR, P, SLOTS], BF16, name="weight", align_bytes=64)
+                weights[i] = weight
+            dst, bank = weights[i][:, side], gain_banks[i, side]
+            if e < LAST:
+                vector.tensor_tensor(
+                    dst,
+                    bank[:].rearrange("p t c -> p c t"),
+                    high_p[e, r // HALF][:, r % HALF].unsqueeze(2).to_broadcast([P, P, SLOTS]),
                     ALU.mult,
                 )
             else:
-                nc.vector.tensor_tensor(
-                    wgs[i][:, ti],
-                    bank[:].rearrange("p t n -> p n t"),
-                    ats[e, tt // H][:, tt % H].unsqueeze(2).to_broadcast([P, P, 4]),
+                vector.tensor_tensor(
+                    dst.rearrange("p (c i) t -> p c t i", i=4),
+                    gained_last[:, :, r, :].rearrange("p t (c i) -> p c t i", i=4),
+                    bank[:, r % HALF, :].rearrange("p (c i) -> p c i", i=4).unsqueeze(2).to_broadcast([P, P // 4, 4, 4]),
                     ALU.mult,
                 )
 
-        def quant_w(i, lo=0, n=2):
-            if lo == 0:
-                w_c = work.tile([P, 2 * P], U32, name="w_c", align_bytes=64, bufs=3)
-                w_s = work.tile([P, 2 * P], U8, name="w_s", align_bytes=64, bufs=3)
-                wq[i] = (w_c, w_s)
-            c, sc = wq[i]
-            cols = slice(lo * P, (lo + n) * P)
-            quant(c[:, cols], sc[:, cols], wgs[i][:, lo : lo + n].rearrange("p a n t -> p (a n t)"))
+        def quantize_weights(i, first=0, count=PAIR):
+            if first == 0:
+                w_codes = work.tile([P, PAIR * P], U32, name="w_codes", align_bytes=64)
+                w_scales = work.tile([P, PAIR * P], U8, name="w_scales", align_bytes=64)
+                weight_codes[i] = (w_codes, w_scales)
+            codes, scales = weight_codes[i]
+            cols = slice(first * P, (first + count) * P)
+            src = weights[i][:, first : first + count]
+            quantize(codes[:, cols], scales[:, cols], src.rearrange("p a c t -> p (a c t)"))
 
-        def lattice(i, ti):
-            e, pr = member(i), pair(i)
-            c, sc = wq[i]
-            if ti == 0:
-                h = work.tile([P, 2, P, 4], F32, name="h", bufs=3)
-                hs[i] = h
-            bank = ps_l.tile([P, 4, P], F32, name="bank_l")
-            cols = slice(ti * P, (ti + 1) * P)
-            for t in range(4):
-                oc = slice(t * P, (t + 1) * P)
-                nc.tensor.matmul_mx(
+        def lattice(i, side):
+            e = member(i)
+            codes, scales = weight_codes[i]
+            if side == 0:
+                h = work.tile([P, PAIR, P, SLOTS], F32, name="h")
+                tanhs[i] = h
+            bank = psum_lattice.tile([P, SLOTS, P], F32, name="lattice_bank")
+            cols = slice(side * P, (side + 1) * P)
+            for t in range(SLOTS):
+                outs = slice(t * P, (t + 1) * P)
+                tensor.matmul_mx(
                     out=bank[:, t, :],
-                    lhsT=th_c[e][:, oc].bitcast(FP8X4),
-                    lhsT_scale=th_s[e][:, oc],
-                    rhs=c[:, cols].bitcast(FP8X4),
-                    rhs_scale=sc[:, cols],
+                    lhsT=theta_codes[e][:, outs].bitcast(FP8X4),
+                    lhsT_scale=theta_scales[e][:, outs],
+                    rhs=codes[:, cols].bitcast(FP8X4),
+                    rhs_scale=scales[:, cols],
                     start=True,
                     stop=True,
                 )
-            nc.scalar.activation(out=hs[i][:, ti], in_=bank[:].rearrange("p t n -> p n t"), func=ACT.Tanh)
+            scalar.activation(out=tanhs[i][:, side], in_=bank[:].rearrange("p t c -> p c t"), func=ACT.Tanh)
 
-        s_ps = ps_s.tile([P, E * 4], F32, name="s_ps")
+        s_gpsimd = keep.tile([P, E * SLOTS], BF16, name="s_gpsimd")
+        s_bank = psum_s.tile([P, E * SLOTS], F32, name="s_bank")
 
-        def gain_f(i, ti, eng):
+        def channel_gain(i, first, end, engine):
             e = member(i)
-            if ti == 0:
-                tail = i >= STEPS - 2
-                f = work.tile([P, 2, P, 4], BF16, name="f", tag=f"f{i}" if tail else "f", align_bytes=64, bufs=1)
-                ffs[i] = f
-            src = sp if eng is nc.gpsimd else s_ps
-            eng.tensor_tensor(
-                ffs[i][:, ti],
-                hs[i][:, ti],
-                src[:, 4 * e : 4 * e + 4].unsqueeze(1).to_broadcast([P, P, 4]),
+            if first == 0:
+                own = f"f{i}" if i >= STEPS - 2 else "f"
+                f = work.tile([P, PAIR * P, SLOTS], BF16, name="f", tag=own, align_bytes=64, bufs=1)
+                channels[i] = f
+            gain = s_gpsimd if engine is gpsimd else s_bank
+            engine.tensor_tensor(
+                channels[i][:, first:end],
+                tanhs[i][:].rearrange("p a c t -> p (a c) t")[:, first:end],
+                gain[:, SLOTS * e : SLOTS * (e + 1)].unsqueeze(1).to_broadcast([P, end - first, SLOTS]),
                 ALU.mult,
             )
 
-        def quant_f(i, lo=0, n=2):
-            if lo == 0:
-                f_c = keep.tile([P, 2 * P], U32, name=f"f_c{i}", align_bytes=64)
-                f_s = keep.tile([P, 2 * P], U8, name=f"f_s{i}", align_bytes=64)
-                fq[i] = (f_c, f_s)
-            c, sc = fq[i]
-            cols = slice(lo * P, (lo + n) * P)
-            quant(c[:, cols], sc[:, cols], ffs[i][:, lo : lo + n].rearrange("p a n t -> p (a n t)"))
+        def quantize_channels(i, first=0, end=PAIR * P):
+            if first == 0:
+                f_codes = keep.tile([P, PAIR * P], U32, name=f"f_codes{i}", align_bytes=64)
+                f_scales = keep.tile([P, PAIR * P], U8, name=f"f_scales{i}", align_bytes=64)
+                channel_codes[i] = (f_codes, f_scales)
+            codes, scales = channel_codes[i]
+            quantize(
+                codes[:, first:end], scales[:, first:end], channels[i][:, first:end].rearrange("p c t -> p (c t)")
+            )
 
-        out_v = out.rearrange("(c t) q -> c t q", t=T)
+        out_rows = out.rearrange("(c r) q -> c r q", r=TILES)
 
-        def mix(tt, e):
-            if e == 0 and tt not in (6, 7):
-                acc = ps_m.tile([P, Q], F32, name="acc", tag="bank_m")
-                accs[tt] = acc
-            elif e == 0:
-                acc_g = ps_g.tile([P, Q], F32, name="acc_g", tag="bank_gb")
-                accs[tt] = acc_g
-            c, sc = fq[tt // 4 * 8 + e * 2 + tt // 2 % 2]
-            cols = slice(tt % 2 * P, (tt % 2 + 1) * P)
-            nc.tensor.matmul_mx(
-                out=accs[tt][:],
-                lhsT=c[:, cols].bitcast(FP8X4),
-                lhsT_scale=sc[:, cols],
-                rhs=v_c[e][:].bitcast(FP8X4),
-                rhs_scale=v_s[e][:],
+        def mix(r, e):
+            if e == 0:
+                pool = psum_gain if r % HALF == HALF - 1 else psum_mixed
+                sum_bank = pool.tile([P, Q], F32, name="sum_bank", tag="bank")
+                sums[r] = sum_bank
+            codes, scales = channel_codes[step_of(r, e)]
+            cols = slice(r % PAIR * P, (r % PAIR + 1) * P)
+            tensor.matmul_mx(
+                out=sums[r][:],
+                lhsT=codes[:, cols].bitcast(FP8X4),
+                lhsT_scale=scales[:, cols],
+                rhs=v_codes[e][:].bitcast(FP8X4),
+                rhs_scale=v_scales[e][:],
                 start=(e == 0),
                 stop=(e == LAST),
             )
 
-        def finish(tt, split=False):
-            res = work.tile([P, Q], F32, name="res", bufs=8)
-            if split:
-                half_q = Q // 2
-                nc.scalar.copy(out=res[:, 0:half_q], in_=accs[tt][:, 0:half_q])
-                nc.sync.dma_start(out=out_v[:, tt, 0:half_q], in_=res[:, 0:half_q])
-                nc.vector.tensor_copy(out=res[:, half_q:Q], in_=accs[tt][:, half_q:Q])
-                nc.sync.dma_start(out=out_v[:, tt, half_q:Q], in_=res[:, half_q:Q])
-            else:
-                nc.scalar.copy(out=res[:], in_=accs[tt][:])
-                nc.sync.dma_start(out=out_v[:, tt, :], in_=res[:])
+        def mix_first(*tiles):
+            for r in tiles:
+                for e in range(LAST):
+                    mix(r, e)
 
-        V, G = nc.vector, nc.gpsimd
-        ca, cb, fa, fb, pa, pb = calibrate(0), calibrate(1), factors(0), factors(1), pieces(0), pieces(1)
-        make_gw(0)
-        for op in (
-            ca[:3] + cb[:1] + ca[3:4] + cb[1:2] + ca[4:5] + cb[2:3]
-            + fa[:1] + pa[:1] + fa[1:3] + pa[1:2] + fa[3:4] + pa[2:4] + fa[4:5] + cb[3:4]
+        def store(r, first, end, copy):
+            copy(out=results[r][:, first:end], in_=sums[r][:, first:end])
+            nc.sync.dma_start(out=out_rows[:, r, first:end], in_=results[r][:, first:end])
+
+        results = {}
+
+        def finish(*tiles, split=False):
+            for r in tiles:
+                mix(r, LAST)
+                result = keep.tile([P, Q], F32, name=f"result{r}")
+                results[r] = result
+                if split:
+                    store(r, 0, Q // 2, scalar.copy)
+                    store(r, Q // 2, Q, vector.tensor_copy)
+                else:
+                    store(r, 0, Q, scalar.copy)
+
+        make_g_weight(0)
+        cal_a, cal_b = calibration(0), calibration(1)
+        low_a, low_b = low_weights(0), low_weights(1)
+        high_a, high_b = high_factors(0), high_factors(1)
+        cal_a[0]()
+        cal_b[0]()
+        vector.tensor_scalar(cal_low[:], cal_bank[:], 2.0, None, ALU.mult)
+        vector.tensor_scalar(cal_high[:], cal_bank[:], -2.0, 2.0, ALU.mult, ALU.add)
+        for call in (
+            cal_a[1:4] + cal_b[1:2] + cal_a[4:5] + cal_b[2:3]
+            + high_a[0:1] + low_a[0:1] + high_a[1:3] + low_a[1:2]
+            + high_a[3:4] + low_a[2:4] + high_a[4:5] + cal_b[3:4]
         ):
-            op()
-        make_aw(0, 0, 0, V)
-        pa[4]()
-        make_aw(0, 0, 1, V)
-        cb[4]()
-        nc.vector.tensor_copy(out=gpf[:], in_=gp[:])
-        make_aw(1, 0, 0, V)
-        make_aw(1, 0, 1, V)
-        for op in pb[:1] + fb[:1] + pb[1:2] + fb[1:3] + pb[2:4] + fb[3:4] + pb[4:] + fb[4:]:
-            op()
-        for t in range(3):
-            theta_group(0, t)
-        make_at(0, 0)
-        make_rt(0)
-        theta_group(0, 3)
+            call()
+        make_high(0, 0, 0)
+        low_a[4]()
+        make_high(0, 0, 1)
+        cal_b[4]()
+        vector.tensor_copy(out=g_last[:], in_=g_last_sb[:])
+        make_high(1, 0, 0)
+        make_high(1, 0, 1)
+        for call in (
+            low_b[0:1] + high_b[0:1] + low_b[1:2] + high_b[1:3] + low_b[2:4] + high_b[3:4] + low_b[4:5] + high_b[4:5]
+        ):
+            call()
+        group_theta(0, 0, 1, 2, 3)
+        make_high_p(0, 0)
+        make_pieces_k(0)
         gains(0)
-        nc.tensor.matmul(s_ps[:], lhsT=idb[:], rhs=sp[:], start=True, stop=True)
-        theta_group(1, 0)
-        theta_group(1, 1)
-        make_at(1, 0)
-        make_gw(1)
+        tensor.matmul(s_bank[:], lhsT=ident[:], rhs=s_sb[:], start=True, stop=True)
+        group_theta(1, 0, 1)
+        make_high_p(1, 0)
+        make_g_weight(1)
 
-        v_g = {}
+        def both_parts(e, half):
+            make_high(e, half, 0)
+            make_high(e, half, 1)
 
-        def v_pack(e):
-            v_g[e] = v_quant(e)
-
-        def v_codes(e):
-            quant(v_c[e][:], v_s[e][:], v_g[e][:].rearrange("p q t -> p (q t)"))
-
-        def th(e, *ts):
-            for t in ts:
-                theta_group(e, t)
-
-        def vw(e, *ts):
-            for t in ts:
-                v_widen(e, t)
-
-        def gsl(h, *ts):
-            for t in ts:
-                make_gs(h, t)
-
-        def mx3(*tts):
-            for tt in tts:
-                for e2 in range(LAST):
-                    mix(tt, e2)
-
-        def fin(*tts):
-            for tt in tts:
-                mix(tt, LAST)
-                finish(tt)
-
-        def aw(e, half):
-            make_aw(e, half, 0, V)
-            make_aw(e, half, 1, V)
-
-        vector_extra = {
-            0: lambda: aw(2, 0),
-            1: lambda: aw(3, 0),
-            3: lambda: aw(0, 1),
-            5: lambda: aw(1, 1),
-            7: lambda: aw(2, 1),
-            8: lambda: v_pack(0),
-            9: lambda: (v_codes(0), aw(3, 1)),
-            10: lambda: v_pack(1),
-            11: lambda: (v_codes(1), v_pack(2)),
-            12: lambda: (v_codes(2), v_pack(3)),
-            13: lambda: v_codes(3),
+        vector_work = {
+            0: lambda: both_parts(2, 0),
+            1: lambda: vector.tensor_copy(out=s_gpsimd[:], in_=s_sb[:]),
+            3: lambda: both_parts(0, 1),
+            5: lambda: (group_theta(3, 3, copy=vector.tensor_copy), both_parts(1, 1)),
+            7: lambda: both_parts(2, 1),
+            8: lambda: group_v(0, 0, Q),
+            9: lambda: (quantize_v(0), both_parts(3, 1)),
+            10: lambda: group_v(1, 0, Q),
+            11: lambda: (quantize_v(1), group_v(2, 0, Q)),
+            12: lambda: (quantize_v(2), group_v(3, Q // 2, Q)),
+            13: lambda: quantize_v(3),
         }
-        extra = {
-            0: lambda: (th(1, 2, 3), make_gw(2)),
-            1: lambda: (make_at(2, 0), th(2, 0, 1)),
-            2: lambda: (gsl(0, 0, 1), th(2, 2, 3)),
-            3: lambda: (gsl(0, 2, 3), th(3, 0, 1)),
-            4: lambda: (th(3, 2, 3), vw(0, 0)),
-            5: lambda: (make_at(0, 1), make_rt(1), vw(0, 1)),
-            6: lambda: (vw(0, 2, 3), vw(1, 0)),
-            7: lambda: (make_at(1, 1), vw(1, 1, 2)),
-            8: lambda: (vw(1, 3), vw(2, 0, 1)),
-            9: lambda: (make_at(2, 1), vw(2, 2, 3)),
-            10: lambda: (gsl(1, 0, 1), vw(3, 0, 1)),
-            11: lambda: (gsl(1, 2, 3), vw(3, 2, 3)),
-            12: lambda: mx3(0),
-            13: lambda: (mx3(1, 2), fin(0, 1, 2)),
-            14: lambda: (mx3(3), fin(3), mx3(4, 5)),
+        scalar_work = {
+            0: lambda: (group_theta(1, 2, 3), make_g_weight(2)),
+            1: lambda: (make_high_p(2, 0), group_theta(2, 0, 1)),
+            2: lambda: (group_theta(2, 2, 3), make_gained_last(0, 0, 1)),
+            3: lambda: (group_theta(3, 0, 1), make_gained_last(0, 2, 3)),
+            4: lambda: (group_theta(3, 2), widen_v(0, 0)),
+            5: lambda: (make_high_p(0, 1), make_pieces_k(1), widen_v(0, 1)),
+            6: lambda: (widen_v(0, 2, 3), widen_v(1, 0)),
+            7: lambda: (make_high_p(1, 1), widen_v(1, 1, 2)),
+            8: lambda: (widen_v(1, 3), widen_v(2, 0, 1)),
+            9: lambda: (make_high_p(2, 1), widen_v(2, 2, 3)),
+            10: lambda: (make_gained_last(1, 0, 1), widen_v(3, 0, 1)),
+            11: lambda: (
+                make_gained_last(1, 2, 3),
+                widen_v(3, 2, 3),
+                group_v(3, 0, Q // 4, copy=scalar.copy),
+                group_v(3, Q // 4, Q // 2, copy=scalar.copy),
+            ),
+            12: lambda: mix_first(0, 1, 2),
+            13: lambda: (mix_first(3), finish(0, 1, 2, 3)),
+            14: lambda: mix_first(4, 5),
         }
-        for k in range(STEPS - 1):
-            product(k, 0)
-            product(k, 1)
-            gains(k + 1)
-            if k >= 2:
-                gain_f(k - 2, 0, V)
-                gain_f(k - 2, 1, V if k == 2 else G)
-            if k % 2 == 0 and k < 8:
-                theta_quant(k // 2)
-            quant_w(k)
-            lattice(k, 0)
-            lattice(k, 1)
-            if k in vector_extra:
-                vector_extra[k]()
-            if k >= 2:
-                quant_f(k - 2)
-            extra[k]()
 
-        k = STEPS - 1
-        for ti in range(2):
-            product(k, ti)
-            quant_w(k, ti, 1)
-            lattice(k, ti)
-        gain_f(k - 2, 0, V)
-        gain_f(k - 2, 1, V)
-        gain_f(k - 1, 0, V)
-        quant_f(k - 2)
-        mx3(6, 7)
-        gain_f(k - 1, 1, V)
-        gain_f(k, 0, V)
-        quant_f(k - 1)
-        fin(4, 5)
-        gain_f(k, 1, V)
-        quant_f(k, 0, 1)
-        quant_f(k, 1, 1)
-        mix(6, LAST)
-        finish(6, split=True)
-        mix(7, LAST)
-        finish(7, split=True)
+        for i in range(STEPS - 1):
+            product(i, 0)
+            product(i, 1)
+            gains(i + 1)
+            if i >= 2:
+                channel_gain(i - 2, 0, VECTOR_COLS, vector)
+                channel_gain(i - 2, VECTOR_COLS, PAIR * P, gpsimd)
+            if i % 2 == 0 and i < STEPS // 2:
+                quantize_theta(member(i))
+            if i == 1:
+                both_parts(3, 0)
+            quantize_weights(i)
+            lattice(i, 0)
+            lattice(i, 1)
+            if i in vector_work:
+                vector_work[i]()
+            if i >= 2:
+                quantize_channels(i - 2)
+            scalar_work[i]()
+
+        end = STEPS - 1
+        product(end, 0)
+        product(end, 1)
+        channel_gain(end - 2, 0, VECTOR_COLS, vector)
+        channel_gain(end - 2, VECTOR_COLS, PAIR * P, gpsimd)
+        for side in range(PAIR):
+            quantize_weights(end, side, 1)
+            lattice(end, side)
+        quantize_channels(end - 2)
+        mix_first(6, 7)
+        channel_gain(end - 1, 0, PAIR * P, vector)
+        channel_gain(end, 0, P, vector)
+        quantize_channels(end - 1)
+        finish(4, 5)
+        channel_gain(end, P, PAIR * P, vector)
+        quantize_channels(end, 0, P)
+        quantize_channels(end, P, PAIR * P)
+        finish(6, 7, split=True)

from contextlib import ExitStack

import concourse.mybir as mybir
from concourse.masks import make_identity

F32 = mybir.dt.float32
BF16 = mybir.dt.bfloat16
U32 = mybir.dt.uint32
U8 = mybir.dt.uint8
FP8 = mybir.dt.float8_e4m3fn
FP8X4 = mybir.dt.float8_e4m3fn_x4
ALU = mybir.AluOpType
ACT = mybir.ActivationFunctionType
AX = mybir.AxisListType

P = 128
SLOTS = 4
N, E, J, NV, O, Q = 1024, 4, 9, 512, 512, 512
TILES = N // P
HALF = TILES // 2
GROUP = HALF * E
PAIR = 2
STEPS = E * TILES // PAIR
LAST = E - 1
SPAN = P // E
VECTOR_COLS = 120
FLOPS = 2 * (E * N * NV * O + N * E * O * Q)


def tile_calibratedlatticeensemble_kernel(tc, x, cal, g, theta, s, v_bytes, v_scale, out):
    nc = tc.nc
    vector, scalar, gpsimd, tensor = nc.vector, nc.scalar, nc.gpsimd, nc.tensor
    with ExitStack() as ctx:
        keep = ctx.enter_context(tc.tile_pool(name="keep", bufs=1))
        work = ctx.enter_context(tc.tile_pool(name="work", bufs=3))
        psum_s = ctx.enter_context(tc.psum_pool(name="psum_s", bufs=1))
        psum_gain = ctx.enter_context(tc.psum_pool(name="psum_gain", bufs=2))
        psum_lattice = ctx.enter_context(tc.psum_pool(name="psum_lattice", bufs=2))
        psum_mixed = ctx.enter_context(tc.psum_pool(name="psum_mixed", bufs=3))
        ctx.enter_context(tc.manual_schedule())

        x_sb = keep.tile([P, TILES * E, J], BF16, name="x_sb")
        nc.sync.dma_start(
            out=x_sb[:].rearrange("p a j -> p (a j)"), in_=x.rearrange("(c r) e j -> c (r e j)", r=TILES)
        )
        rows_sb = keep.tile([P, NV + E * J], BF16, name="rows_sb")
        vector.memset(rows_sb[:], 0.0)
        nc.sync.dma_start(out=rows_sb[0:1, NV : NV + E * J], in_=cal.rearrange("(o e) j -> o (e j)", o=1))
        nc.sync.dma_start(out=rows_sb[0:E, 0:NV], in_=g)
        s_sb = keep.tile([P, E * SLOTS], BF16, name="s_sb")
        v_scale_sb = keep.tile([P, E, SLOTS], F32, name="v_scale_sb")
        g_last_sb = keep.tile([P, SLOTS], BF16, name="g_last_sb")
        theta_sb, v_bytes_sb = [], []
        for e in range(E):
            theta_sb.append(keep.tile([P, SLOTS, O], BF16, name=f"theta_sb{e}"))
            v_bytes_sb.append(keep.tile([P, SLOTS, Q], U8, name=f"v_bytes_sb{e}", align_bytes=64))

        def load_theta(e):
            nc.sync.dma_start(
                out=theta_sb[e][:].rearrange("p j o -> p (j o)"),
                in_=theta[e].rearrange("(p j) o -> p (j o)", j=SLOTS),
            )

        load_theta(0)
        load_theta(1)
        nc.sync.dma_start(
            out=s_sb[:].rearrange("p (e t) -> p e t", t=SLOTS), in_=s.rearrange("(e p t) -> p e t", p=P, t=SLOTS)
        )
        nc.sync.dma_start(out=g_last_sb[:], in_=g[LAST].rearrange("(p t) -> p t", t=SLOTS))
        load_theta(2)
        load_theta(3)
        nc.sync.dma_start(out=v_scale_sb[:], in_=v_scale.rearrange("(e p t) o -> p e (t o)", p=P, t=SLOTS))
        for e in range(E):
            nc.sync.dma_start(
                out=v_bytes_sb[e][:].rearrange("p t q -> p (t q)"),
                in_=v_bytes[e * O : (e + 1) * O, :].rearrange("(p t) q -> p (t q)", t=SLOTS),
            )

        ident_f32 = keep.tile([P, P], F32, name="ident_f32")
        make_identity(nc, ident_f32[:])
        pieces = keep.tile([P, TILES, P], BF16, name="pieces")
        gpsimd.memset(pieces[:], 0.0)
        ident = keep.tile([P, P], BF16, name="ident")
        vector.tensor_copy(out=ident[:], in_=ident_f32[:])
        row_mask = keep.tile([P, E * SLOTS], F32, name="row_mask")
        vector.tensor_reduce(
            out=row_mask[:].rearrange("k (e t) -> k e t", t=SLOTS),
            in_=ident_f32[:].rearrange("k (e d t) -> k e t d", e=E, t=SLOTS),
            axis=AX.X,
            op=ALU.add,
        )
        spread = keep.tile([P, E, SPAN], BF16, name="spread")
        vector.tensor_copy(out=spread[:], in_=ident[:, 0:E].unsqueeze(2).to_broadcast([P, E, SPAN]))

        cal_bank = psum_mixed.tile([P, E * J], F32, name="cal_bank", tag="bank")
        tensor.matmul(
            cal_bank[:],
            lhsT=ident[:, 0:1].to_broadcast([P, P]),
            rhs=rows_sb[:, NV : NV + E * J],
            start=True,
            stop=True,
        )
        g_bank = psum_mixed.tile([P, NV], F32, name="g_bank", tag="bank")
        tensor.matmul(
            g_bank[:], lhsT=spread[:].rearrange("k e d -> k (e d)"), rhs=rows_sb[:, 0:NV], start=True, stop=True
        )
        g_rows = keep.tile([P, SLOTS, P], BF16, name="g_rows")
        scalar.copy(out=g_rows[:], in_=g_bank[:].rearrange("k (p t) -> k t p", t=SLOTS))

        cal_low = keep.tile([P, E * J], F32, name="cal_low")
        cal_high = keep.tile([P, E * J], F32, name="cal_high")
        above = keep.tile([P, TILES, E * J], F32, name="above")
        part_low = keep.tile([P, TILES, E * J], F32, name="part_low")
        part_high = keep.tile([P, TILES, E * J], F32, name="part_high")
        factor = keep.tile([P, 2, TILES * E, J], F32, name="factor")
        low = keep.tile([P, TILES * E, 4], F32, name="low")
        remainder = keep.tile([P, TILES * E, 4], F32, name="remainder")
        bits01 = keep.tile([P, TILES * E, 4], F32, name="bits01")
        bits23 = keep.tile([P, TILES * E, 4], F32, name="bits23")
        bits45 = keep.tile([P, TILES * E, 4], F32, name="bits45")
        bits0123 = keep.tile([P, TILES * E, 16], F32, name="bits0123")
        bits456 = keep.tile([P, TILES * E, 8], F32, name="bits456")
        x_rows = x_sb[:].rearrange("p (r e) j -> p r (e j)", r=TILES)
        factor_flat = factor[:].rearrange("p b a j -> p b (a j)")
        piece = pieces[:].rearrange("p r (e k) -> p (r e) k", k=SPAN)

        def calibration(half):
            ts = slice(half * HALF, (half + 1) * HALF)
            fs = slice(half * GROUP * J, (half + 1) * GROUP * J)
            full = [P, HALF, E * J]
            return [
                lambda: vector.tensor_scalar(above[:, ts], x_rows[:, ts], 0.5, 0.5, ALU.max, ALU.subtract),
                lambda: vector.scalar_tensor_tensor(
                    part_low[:, ts], x_rows[:, ts], 0.5, cal_low[:].unsqueeze(1).to_broadcast(full), ALU.min, ALU.mult
                ),
                lambda: vector.tensor_tensor(
                    part_high[:, ts], above[:, ts], cal_high[:].unsqueeze(1).to_broadcast(full), ALU.mult
                ),
                lambda: vector.tensor_tensor(
                    factor_flat[:, 1, fs],
                    part_low[:, ts].rearrange("p r c -> p (r c)"),
                    part_high[:, ts].rearrange("p r c -> p (r c)"),
                    ALU.add,
                ),
                lambda: vector.tensor_scalar(
                    factor_flat[:, 0, fs], factor_flat[:, 1, fs], -1.0, 1.0, ALU.mult, ALU.add
                ),
            ]

        def outer(dst, a, b, na, nb):
            full = [P, GROUP, na, nb]
            vector.tensor_tensor(
                dst.rearrange("p g (a b) -> p g a b", b=nb),
                a.unsqueeze(3).to_broadcast(full),
                b.unsqueeze(2).to_broadcast(full),
                ALU.mult,
            )

        def bit_pair(half, j):
            return factor[:, :, half * GROUP : (half + 1) * GROUP, j].rearrange("p b a -> p a b")

        def low_weights(half):
            rs = slice(half * GROUP, (half + 1) * GROUP)
            return [
                lambda: outer(low[:, rs], bit_pair(half, 7), bit_pair(half, 8), 2, 2),
                lambda: vector.tensor_copy(out=piece[:, rs, 0:4], in_=low[:, rs]),
                lambda: vector.tensor_tensor(remainder[:, rs], low[:, rs], piece[:, rs, 0:4], ALU.subtract),
                lambda: vector.tensor_tensor(piece[:, rs, 4:8], low[:, rs], piece[:, rs, 0:4], ALU.subtract),
                lambda: vector.tensor_tensor(piece[:, rs, 8:12], remainder[:, rs], piece[:, rs, 4:8], ALU.subtract),
            ]

        def high_factors(half):
            rs = slice(half * GROUP, (half + 1) * GROUP)
            return [
                lambda: outer(bits01[:, rs], bit_pair(half, 0), bit_pair(half, 1), 2, 2),
                lambda: outer(bits23[:, rs], bit_pair(half, 2), bit_pair(half, 3), 2, 2),
                lambda: outer(bits45[:, rs], bit_pair(half, 4), bit_pair(half, 5), 2, 2),
                lambda: outer(bits0123[:, rs], bits01[:, rs], bits23[:, rs], 4, 4),
                lambda: outer(bits456[:, rs], bits45[:, rs], bit_pair(half, 6), 4, 2),
            ]

        g_weight = keep.tile([P, LAST, SLOTS, P], BF16, name="g_weight")

        def make_g_weight(e):
            for t in range(SLOTS):
                scalar.activation(
                    out=g_weight[:, e, t, :],
                    in_=g_rows[:, t, :],
                    func=ACT.Copy,
                    scale=row_mask[:, SLOTS * e + t : SLOTS * e + t + 1],
                )

        pieces_k = keep.tile([P, TILES, P], BF16, name="pieces_k")

        def make_pieces_k(half):
            bank = psum_mixed.tile([P, HALF, P], BF16, name="piece_bank", tag="bank")
            for i in range(HALF):
                tensor.transpose(bank[:, i, :], pieces[:, HALF * half + i, :], ident[:])
            scalar.copy(out=pieces_k[:, HALF * half : HALF * (half + 1), :], in_=bank[:])

        gained_last = keep.tile([P, SLOTS, TILES, P], F32, name="gained_last")
        g_last = keep.tile([P, SLOTS], F32, name="g_last")

        def make_gained_last(half, *slots):
            for t in slots:
                bank = psum_mixed.tile([P, HALF, P], F32, name="low_bank", tag="bank")
                for i in range(HALF):
                    row = (HALF * half + i) * E + LAST
                    tensor.transpose(bank[:, i, :], low[:, row, t : t + 1].to_broadcast([P, P]), ident_f32[:])
                scalar.activation(
                    out=gained_last[:, t, HALF * half : HALF * (half + 1), :],
                    in_=bank[:],
                    func=ACT.Copy,
                    scale=g_last[:, t : t + 1],
                )

        high_rows, high_p = {}, {}

        def make_high(e, half, part):
            if part == 0:
                high_tile = keep.tile([P, HALF, 16, 8], F32, name=f"high_{e}_{half}")
                high_rows[e, half] = high_tile
            full = [P, PAIR, 16, 8]
            rs = slice(half * HALF + PAIR * part, half * HALF + PAIR * (part + 1))
            vector.tensor_tensor(
                high_rows[e, half][:, PAIR * part : PAIR * (part + 1)],
                bits0123[:].rearrange("p (r e) a -> p r e a", e=E)[:, rs, e, :].unsqueeze(3).to_broadcast(full),
                bits456[:].rearrange("p (r e) b -> p r e b", e=E)[:, rs, e, :].unsqueeze(2).to_broadcast(full),
                ALU.mult,
            )

        def high_of(e, r):
            return high_rows[e, r // HALF][:, r % HALF].rearrange("p a b -> p (a b)")

        def make_high_p(e, half):
            bank = psum_mixed.tile([P, HALF, P], F32, name="high_bank", tag="bank")
            for i in range(HALF):
                tensor.transpose(bank[:, i, :], high_of(e, half * HALF + i), ident_f32[:])
            high_p_tile = keep.tile([P, HALF, P], F32, name=f"high_p_{e}_{half}")
            scalar.copy(out=high_p_tile[:], in_=bank[:])
            high_p[e, half] = high_p_tile

        def quantize(codes, scales, src):
            vector.quantize_mx(out=codes.bitcast(FP8X4), scales=scales, in_=src)

        theta_codes, theta_scales, theta_grouped = [], [], []
        v_codes, v_scales, v_wide, v_grouped = [], [], [], []
        for e in range(E):
            theta_codes.append(keep.tile([P, O], U32, name=f"theta_codes{e}", align_bytes=64))
            theta_scales.append(keep.tile([P, O], U8, name=f"theta_scales{e}", align_bytes=64))
            theta_grouped.append(keep.tile([P, SLOTS, P, SLOTS], BF16, name=f"theta_grouped{e}", align_bytes=64))
            v_codes.append(keep.tile([P, Q], U32, name=f"v_codes{e}", align_bytes=64))
            v_scales.append(keep.tile([P, Q], U8, name=f"v_scales{e}", align_bytes=64))
            v_wide.append(keep.tile([P, SLOTS, Q], BF16, name=f"v_wide{e}"))
            v_grouped.append(keep.tile([P, Q, SLOTS], BF16, name=f"v_grouped{e}", align_bytes=64))

        def group_theta(e, *quarters, copy=scalar.copy):
            for i in quarters:
                ms = slice(P // 4 * i, P // 4 * (i + 1))
                copy(
                    out=theta_grouped[e][:, :, ms, :].rearrange("p t m j -> p m t j"),
                    in_=theta_sb[e][:].rearrange("p j (m t) -> p m t j", t=SLOTS)[:, ms],
                )

        def quantize_theta(e):
            quantize(theta_codes[e][:], theta_scales[e][:], theta_grouped[e][:].rearrange("p t m j -> p (t m j)"))

        def widen_v(e, *slots):
            for t in slots:
                scalar.activation(
                    out=v_wide[e][:, t, :],
                    in_=v_bytes_sb[e][:, t, :].bitcast(FP8),
                    func=ACT.Copy,
                    scale=v_scale_sb[:, e, t : t + 1],
                )

        def group_v(e, first, end, copy=vector.tensor_copy):
            copy(
                out=v_grouped[e][:, first:end].rearrange("p (c i) t -> p c t i", i=4),
                in_=v_wide[e][:, :, first:end].rearrange("p t (c i) -> p c t i", i=4),
            )

        def quantize_v(e):
            quantize(v_codes[e][:], v_scales[e][:], v_grouped[e][:].rearrange("p q t -> p (q t)"))

        gain_banks, weights, weight_codes, tanhs, channels, channel_codes, sums = {}, {}, {}, {}, {}, {}, {}

        def member(i):
            return i % (STEPS // 2) // 2

        def row_tile(i, side):
            return i // (STEPS // 2) * HALF + i % 2 * PAIR + side

        def step_of(r, e):
            return r // HALF * (STEPS // 2) + e * 2 + r // PAIR % 2

        def gains(i):
            e = member(i)
            if e < LAST:
                for side in range(PAIR):
                    gain_bank = psum_gain.tile([P, SLOTS, P], F32, name="gain_bank", tag="bank")
                    for t in range(SLOTS):
                        tensor.matmul(
                            gain_bank[:, t, :],
                            lhsT=g_weight[:, e, t, :],
                            rhs=pieces_k[:, row_tile(i, side), :],
                            start=True,
                            stop=True,
                        )
                    gain_banks[i, side] = gain_bank
            elif i % 2 == 0:
                last_bank = psum_gain.tile([P, HALF, P], F32, name="last_bank", tag="bank")
                for j in range(HALF):
                    tensor.transpose(last_bank[:, j, :], high_of(e, row_tile(i, j)), ident_f32[:])
                    gain_banks[i + j // PAIR, j % PAIR] = last_bank

        def product(i, side):
            e, r = member(i), row_tile(i, side)
            if side == 0:
                weight = work.tile([P, PAIR, P, SLOTS], BF16, name="weight", align_bytes=64)
                weights[i] = weight
            dst, bank = weights[i][:, side], gain_banks[i, side]
            if e < LAST:
                vector.tensor_tensor(
                    dst,
                    bank[:].rearrange("p t c -> p c t"),
                    high_p[e, r // HALF][:, r % HALF].unsqueeze(2).to_broadcast([P, P, SLOTS]),
                    ALU.mult,
                )
            else:
                vector.tensor_tensor(
                    dst.rearrange("p (c i) t -> p c t i", i=4),
                    gained_last[:, :, r, :].rearrange("p t (c i) -> p c t i", i=4),
                    bank[:, r % HALF, :].rearrange("p (c i) -> p c i", i=4).unsqueeze(2).to_broadcast([P, P // 4, 4, 4]),
                    ALU.mult,
                )

        def quantize_weights(i, first=0, count=PAIR):
            if first == 0:
                w_codes = work.tile([P, PAIR * P], U32, name="w_codes", align_bytes=64)
                w_scales = work.tile([P, PAIR * P], U8, name="w_scales", align_bytes=64)
                weight_codes[i] = (w_codes, w_scales)
            codes, scales = weight_codes[i]
            cols = slice(first * P, (first + count) * P)
            src = weights[i][:, first : first + count]
            quantize(codes[:, cols], scales[:, cols], src.rearrange("p a c t -> p (a c t)"))

        def lattice(i, side):
            e = member(i)
            codes, scales = weight_codes[i]
            if side == 0:
                h = work.tile([P, PAIR, P, SLOTS], F32, name="h")
                tanhs[i] = h
            bank = psum_lattice.tile([P, SLOTS, P], F32, name="lattice_bank")
            cols = slice(side * P, (side + 1) * P)
            for t in range(SLOTS):
                outs = slice(t * P, (t + 1) * P)
                tensor.matmul_mx(
                    out=bank[:, t, :],
                    lhsT=theta_codes[e][:, outs].bitcast(FP8X4),
                    lhsT_scale=theta_scales[e][:, outs],
                    rhs=codes[:, cols].bitcast(FP8X4),
                    rhs_scale=scales[:, cols],
                    start=True,
                    stop=True,
                )
            scalar.activation(out=tanhs[i][:, side], in_=bank[:].rearrange("p t c -> p c t"), func=ACT.Tanh)

        s_gpsimd = keep.tile([P, E * SLOTS], BF16, name="s_gpsimd")
        s_bank = psum_s.tile([P, E * SLOTS], F32, name="s_bank")

        def channel_gain(i, first, end, engine):
            e = member(i)
            if first == 0:
                own = f"f{i}" if i >= STEPS - 2 else "f"
                f = work.tile([P, PAIR * P, SLOTS], BF16, name="f", tag=own, align_bytes=64, bufs=1)
                channels[i] = f
            gain = s_gpsimd if engine is gpsimd else s_bank
            engine.tensor_tensor(
                channels[i][:, first:end],
                tanhs[i][:].rearrange("p a c t -> p (a c) t")[:, first:end],
                gain[:, SLOTS * e : SLOTS * (e + 1)].unsqueeze(1).to_broadcast([P, end - first, SLOTS]),
                ALU.mult,
            )

        def quantize_channels(i, first=0, end=PAIR * P):
            if first == 0:
                f_codes = keep.tile([P, PAIR * P], U32, name=f"f_codes{i}", align_bytes=64)
                f_scales = keep.tile([P, PAIR * P], U8, name=f"f_scales{i}", align_bytes=64)
                channel_codes[i] = (f_codes, f_scales)
            codes, scales = channel_codes[i]
            quantize(
                codes[:, first:end], scales[:, first:end], channels[i][:, first:end].rearrange("p c t -> p (c t)")
            )

        out_rows = out.rearrange("(c r) q -> c r q", r=TILES)

        def mix(r, e):
            if e == 0:
                pool = psum_gain if r % HALF == HALF - 1 else psum_mixed
                sum_bank = pool.tile([P, Q], F32, name="sum_bank", tag="bank")
                sums[r] = sum_bank
            codes, scales = channel_codes[step_of(r, e)]
            cols = slice(r % PAIR * P, (r % PAIR + 1) * P)
            tensor.matmul_mx(
                out=sums[r][:],
                lhsT=codes[:, cols].bitcast(FP8X4),
                lhsT_scale=scales[:, cols],
                rhs=v_codes[e][:].bitcast(FP8X4),
                rhs_scale=v_scales[e][:],
                start=(e == 0),
                stop=(e == LAST),
            )

        def mix_first(*tiles):
            for r in tiles:
                for e in range(LAST):
                    mix(r, e)

        def store(r, first, end, copy):
            copy(out=results[r][:, first:end], in_=sums[r][:, first:end])
            nc.sync.dma_start(out=out_rows[:, r, first:end], in_=results[r][:, first:end])

        results = {}

        def finish(*tiles, split=False):
            for r in tiles:
                mix(r, LAST)
                result = keep.tile([P, Q], F32, name=f"result{r}")
                results[r] = result
                if split:
                    store(r, 0, Q // 2, scalar.copy)
                    store(r, Q // 2, Q, vector.tensor_copy)
                else:
                    store(r, 0, Q, scalar.copy)

        make_g_weight(0)
        cal_a, cal_b = calibration(0), calibration(1)
        low_a, low_b = low_weights(0), low_weights(1)
        high_a, high_b = high_factors(0), high_factors(1)
        cal_a[0]()
        cal_b[0]()
        vector.tensor_scalar(cal_low[:], cal_bank[:], 2.0, None, ALU.mult)
        vector.tensor_scalar(cal_high[:], cal_bank[:], -2.0, 2.0, ALU.mult, ALU.add)
        for call in (
            cal_a[1:4] + cal_b[1:2] + cal_a[4:5] + cal_b[2:3]
            + high_a[0:1] + low_a[0:1] + high_a[1:3] + low_a[1:2]
            + high_a[3:4] + low_a[2:4] + high_a[4:5] + cal_b[3:4]
        ):
            call()
        make_high(0, 0, 0)
        low_a[4]()
        make_high(0, 0, 1)
        cal_b[4]()
        vector.tensor_copy(out=g_last[:], in_=g_last_sb[:])
        make_high(1, 0, 0)
        make_high(1, 0, 1)
        for call in (
            low_b[0:1] + high_b[0:1] + low_b[1:2] + high_b[1:3] + low_b[2:4] + high_b[3:4] + low_b[4:5] + high_b[4:5]
        ):
            call()
        group_theta(0, 0, 1, 2, 3)
        make_high_p(0, 0)
        make_pieces_k(0)
        gains(0)
        tensor.matmul(s_bank[:], lhsT=ident[:], rhs=s_sb[:], start=True, stop=True)
        group_theta(1, 0, 1)
        make_high_p(1, 0)
        make_g_weight(1)

        def both_parts(e, half):
            make_high(e, half, 0)
            make_high(e, half, 1)

        vector_work = {
            0: lambda: both_parts(2, 0),
            1: lambda: vector.tensor_copy(out=s_gpsimd[:], in_=s_sb[:]),
            3: lambda: both_parts(0, 1),
            5: lambda: (group_theta(3, 3, copy=vector.tensor_copy), both_parts(1, 1)),
            7: lambda: both_parts(2, 1),
            8: lambda: group_v(0, 0, Q),
            9: lambda: (quantize_v(0), both_parts(3, 1)),
            10: lambda: group_v(1, 0, Q),
            11: lambda: (quantize_v(1), group_v(2, 0, Q)),
            12: lambda: (quantize_v(2), group_v(3, Q // 2, Q)),
            13: lambda: quantize_v(3),
        }
        scalar_work = {
            0: lambda: (group_theta(1, 2, 3), make_g_weight(2)),
            1: lambda: (make_high_p(2, 0), group_theta(2, 0, 1)),
            2: lambda: (group_theta(2, 2, 3), make_gained_last(0, 0, 1)),
            3: lambda: (group_theta(3, 0, 1), make_gained_last(0, 2, 3)),
            4: lambda: (group_theta(3, 2), widen_v(0, 0)),
            5: lambda: (make_high_p(0, 1), make_pieces_k(1), widen_v(0, 1)),
            6: lambda: (widen_v(0, 2, 3), widen_v(1, 0)),
            7: lambda: (make_high_p(1, 1), widen_v(1, 1, 2)),
            8: lambda: (widen_v(1, 3), widen_v(2, 0, 1)),
            9: lambda: (make_high_p(2, 1), widen_v(2, 2, 3)),
            10: lambda: (make_gained_last(1, 0, 1), widen_v(3, 0, 1)),
            11: lambda: (
                make_gained_last(1, 2, 3),
                widen_v(3, 2, 3),
                group_v(3, 0, Q // 4, copy=scalar.copy),
                group_v(3, Q // 4, Q // 2, copy=scalar.copy),
            ),
            12: lambda: mix_first(0, 1, 2),
            13: lambda: (mix_first(3), finish(0, 1, 2, 3)),
            14: lambda: mix_first(4, 5),
        }

        for i in range(STEPS - 1):
            product(i, 0)
            product(i, 1)
            gains(i + 1)
            if i >= 2:
                channel_gain(i - 2, 0, VECTOR_COLS, vector)
                channel_gain(i - 2, VECTOR_COLS, PAIR * P, gpsimd)
            if i % 2 == 0 and i < STEPS // 2:
                quantize_theta(member(i))
            if i == 1:
                both_parts(3, 0)
            quantize_weights(i)
            lattice(i, 0)
            lattice(i, 1)
            if i in vector_work:
                vector_work[i]()
            if i >= 2:
                quantize_channels(i - 2)
            scalar_work[i]()

        end = STEPS - 1
        product(end, 0)
        product(end, 1)
        channel_gain(end - 2, 0, VECTOR_COLS, vector)
        channel_gain(end - 2, VECTOR_COLS, PAIR * P, gpsimd)
        for side in range(PAIR):
            quantize_weights(end, side, 1)
            lattice(end, side)
        quantize_channels(end - 2)
        mix_first(6, 7)
        channel_gain(end - 1, 0, PAIR * P, vector)
        channel_gain(end, 0, P, vector)
        quantize_channels(end - 1)
        finish(4, 5)
        channel_gain(end, P, PAIR * P, vector)
        quantize_channels(end, 0, P)
        quantize_channels(end, P, PAIR * P)
        finish(6, 7, split=True)
